import numpy as np, ml_dtypes
CORES = [2,3,42,43,82,83,122,123]
N = 8
import mx_ref
BF = ml_dtypes.bfloat16
def gentries(a):
    return np.ascontiguousarray(a.reshape(8, 16, -1).transpose(0, 2, 1)).reshape(8, -1)
def gtable(e):
    e = np.asarray(e); return np.ascontiguousarray(e.reshape(8, -1, 16).transpose(0, 2, 1)).reshape(128, -1).astype(np.int32)
def gcols(t, e):
    v = np.concatenate([t.reshape(8, 16, -1, 4), np.zeros((8, 16, 1, 4), BF)], axis=2)
    return np.ascontiguousarray(np.stack([v[g][:, e[g]] for g in range(8)])).reshape(128, -1)
def gpick(z, e):
    return np.concatenate([z[16 * g:16 * g + 16][:, e[g]] for g in range(8)])
def tile(rs):
    return np.stack(rs, axis=2).reshape(128, -1).astype(BF)
def pick(q, e):
    c = np.concatenate([q[0].reshape(128, -1, 4), np.zeros((128, 1, 4), np.uint8)], axis=1); s = np.concatenate([q[1], np.ones((16, 1), np.uint8)], axis=1)
    return (np.ascontiguousarray(c[:, e].reshape(128, -1)), np.ascontiguousarray(s[:, e]))
def join(*qs):
    return (np.concatenate([q[0] for q in qs], axis=1), np.concatenate([q[1] for q in qs], axis=1))
def put(q, e, v):
    c, s = q[0].reshape(128, -1, 4).copy(), q[1].copy(); c[:, e] = v[0].reshape(128, -1, 4); s[:, e] = v[1]
    return (c.reshape(128, -1), s)
def pk(c, s):
    return (np.ascontiguousarray(c), mx_ref.live(s))
def emit(q):
    return q[0], q[1]
def packed(v, rng):
    q = [mx_ref.quantize(np.ascontiguousarray(v[r])) for r in range(N)]
    return np.stack([a for a, b in q]), np.stack([mx_ref.plane(b, rng) for a, b in q])
def values_of_codes():
    e, c = np.zeros((128, 128, 4), np.float32), np.zeros((128, 2, 4), np.uint8)
    e[np.arange(128), np.arange(128), 0] = 1
    c[:127, :, 0] = np.arange(256).reshape(2, 128).T[:127]
    return mx_ref.matmul(mx_ref.quantize(e.reshape(128, 512).astype(BF)), (c.reshape(128, 8), np.full((16, 2), 127, np.uint8))).T.reshape(-1).astype(np.float64)
CODE_VALUE, SCALE_VALUE = values_of_codes(), 2.0 ** (np.arange(256) - 127.0)
def decode(q):
    return (CODE_VALUE[q[0]].reshape(16, 8, -1, 4) * SCALE_VALUE[q[1]][:, None, :, None] + 0.0).reshape(128, -1).astype(np.float32)
def f(rng, *shape):
    return mx_ref.flush((rng.standard_normal(shape, dtype=np.float32) * np.exp2(rng.integers(-2, 3, shape[:-1] + (1,)))).astype(BF))
def wide(rng, *shape, cols=0):
    v = rng.standard_normal(shape, dtype=np.float32) * np.exp2(rng.integers(-12, 13, shape)).astype(np.float32)
    if cols: v *= np.repeat(np.exp2(rng.integers(-cols, cols + 1, shape[:-2] + (1, shape[-1] // 4))) * (rng.random(shape[:-2] + (1, shape[-1] // 4)) > 0.0625), 4, axis=-1).astype(np.float32)
    return mx_ref.flush(v.astype(BF))
C = 320
STEP = [1, 2, 4]
def numbers_of(rng):
    return {"x": np.array(f(rng, N, 128, 4 * C)), "u": np.array(f(rng, N, 128, 512)), "v": np.array(f(rng, N, 128, 512))}
def orders(rng):
    return rng.permuted(np.tile(np.arange(C), (N, 8, 1)), axis=2)
def mates(rng):
    e = orders(rng)
    m = np.zeros_like(e)
    np.put_along_axis(m, e[:, :, 0::2], e[:, :, 1::2], axis=2)
    np.put_along_axis(m, e[:, :, 1::2], e[:, :, 0::2], axis=2)
    return m
def stored(c, a, m):
    return {"cl": np.stack([gtable(c[r]) for r in range(N)]), "pl": np.stack([gtable(a[r]) for r in range(N)]), "ml": np.stack([gtable(m[r]) for r in range(N)])}
def lists(rng):
    return stored(orders(rng), orders(rng), mates(rng))
def layers(rng, still=[]):
    w = np.array(f(rng, N, 128, 2048)).reshape(N, 8, 16, 4, 8, 16, 4)
    for i in still:
        w[:, :, i] = 0
        w[:, :, :, :, :, i] = 0
    return w
def weights(rng, w):
    c, s = packed(np.ascontiguousarray(w).reshape(N, 128, 2048), rng)
    return {"wc": c, "ws": s}
def setup_inputs(rng):
    return {**numbers_of(rng), **lists(rng), **weights(rng, layers(rng))}
def setup_inputs_ties(rng):
    d = numbers_of(rng)
    o = rng.permutation(N)
    k = rng.integers(0, 4, (N, 8, C))
    k[o[1]] -= 4
    k[o[2], rng.permutation(8)[:4]] = 1
    x = d["x"].reshape(N, 8, 16, C, 4)
    x[:, :, 0] = 0
    x[:, :, 0, :, 0] = k.astype(np.float32).astype(BF)
    u = d["u"].reshape(N, 128, 128, 4)
    u[:, :, ::16] = 0
    for r in range(N):
        for h in range(0, 128, 16): u[r, h, h, 0] = 0.0 if r == o[0] else 1.0
    c, a, m = orders(rng), orders(rng), mates(rng)
    c[o[3]] = m[o[3]]
    return {"x": x.reshape(N, 128, 4 * C), "u": u.reshape(N, 128, 512), "v": d["v"], **stored(c, a, m), **weights(rng, layers(rng, [0]))}
def setup_inputs_near(rng):
    d = numbers_of(rng)
    x = d["x"].astype(np.float32).reshape(N, 8, 16, C, 4)
    x[:, :, 0] = 0
    x[:, :, 8:] = 0
    u = d["u"].reshape(N, 128, 128, 4)
    u[:, :, ::16] = 0
    o = (np.arange(N) + rng.integers(4)) % 4
    for r in range(N):
        c = rng.choice([-1.0, 1.0], (8, 1))
        s = rng.integers(0, 16, (8, C))
        digits = ((s[:, :, None] >> np.arange(4)) & 1) * np.exp2(np.arange(4) - 23.0)
        if o[r] < 2:
            x[r, :, 0, :, 0] = c
            x[r, :, 8] = digits
            x[r, :, 11, :, 0] = 2.0 ** -10
        elif o[r] == 2: x[r, :, 8] = digits * rng.choice([-1.0, 1.0], (8, C, 1))
        else:
            x[r, :, 8, :, 0] = np.where(s < 8, 1.25, 0.0) * 2.0 ** -29 * c
            x[r, :, 9, :, 0] = np.where(s < 8, 0.0, 1.125) * 2.0 ** -29 * c
            for g in rng.permutation(8)[:4]:
                e = rng.choice([-1.0, 1.0], C) * 2.0 ** -29
                x[r, g, 8, :, 0] = 1.25 * e
                x[r, g, 9, :, 0] = -1.125 * e
        if o[r] >= 2: x[r, :, 12, :, 0] = np.where(rng.random((8, C)) < 0.5, 1.0, 1.5) * 2.0 ** -30
        at = [0, C - 1, int(rng.integers(C)), int(rng.integers(C))]
        for g, j in zip(rng.permutation(8)[:4], at): x[r, g, 0, j, 0] = 2.0 ** 29 * rng.choice([-1.0, 1.0])
        k = 1.0 if o[r] == 0 else 2.0 ** -30
        for h in range(0, 128, 16):
            u[r, h, h, 0] = k if o[r] < 2 else 1.0
            if o[r] < 2: u[r, h + 11, h, 0] = k
            if o[r] < 3: u[r, h + 8, h] = k
            else:
                u[r, h + 8, h, 0] = k
                u[r, h + 9, h, 0] = 1.125 * k
                u[r, h + 10, h, 0] = k
    w = layers(rng, [0, 8, 9, 10, 11, 12, 13, 14, 15])
    for g in range(8): w[:, g, 12, 0, g, 10, 0] = 2.0 ** -8
    return {"x": x.reshape(N, 128, 4 * C).astype(BF), "u": u.reshape(N, 128, 512), "v": d["v"], **lists(rng), **weights(rng, w)}
def setup_inputs_odd(rng):
    d = numbers_of(rng)
    k = (N, 8, 2, 8, C, 4)
    x = (1.0 + (2 * rng.integers(0, 64, k) + 1) * 2.0 ** -7) * np.exp2(-rng.integers(0, 7, k).astype(np.float64)) * rng.choice([-1.0, 1.0], k)
    x[:, :, 0, 0, :, 0] = 1.96875 * 2.0 ** 8 * rng.choice([-1.0, 1.0], (N, 8, C))
    x[:, :, 1, 0, :, 0] = np.where(rng.random((N, 8, C)) < 0.5, 1.875, 0.09375) * 2.0 ** 8
    u = d["u"].reshape(N, 8, 2, 8, 128, 4)
    u[:, :, :, 0, ::16] = 0
    for r in range(N):
        for i, g in enumerate(rng.permutation(8)[:4]):
            x[r, g, 0, 1, :, 0] = (8 + rng.integers(0, 2, C)) * 2.0 ** (i - 8)
            u[r, :, :, :, 16 * g] = 0
            u[r, g, 0, 1, 16 * g, 0] = 1.0
    return {"x": x.astype(np.float32).reshape(N, 128, 4 * C).astype(BF), "u": u.reshape(N, 128, 512), "v": d["v"], **lists(rng), **weights(rng, layers(rng, [0, 8]))}
def setup_inputs_ends(rng):
    d = numbers_of(rng)
    x = np.zeros((N, 8, 16, C, 4))
    u = d["u"].astype(np.float32).reshape(N, 128, 128, 4)
    v = d["v"].astype(np.float32)
    w = np.zeros((N, 128, 4, 128, 4), np.float32)
    o, e = rng.permutation(N) % 4, rng.permutation(N) % 4
    i = np.arange(128)
    for r in range(N):
        h = rng.permutation(8)
        s = np.where(h < 2, 0.0, h % 2 * 2.0 - 1.0)[None, :, None]
        high = (0.9 + 0.1 * rng.random((8, 16, C, 4))) * 2.0 ** 30
        if o[r] == 0: x[r] = -high
        if o[r] == 1: x[r] = high * rng.choice([-1.0, 1.0], (1, 1, C, 1))
        if o[r] == 2: x[r] = -(1.0 + 0.125 * rng.integers(0, 8, (8, 16, C, 4))) * 2.0 ** -30
        if o[r] == 3: x[r] = d["x"][r].astype(np.float32).reshape(8, 16, C, 4)[:, :, :1]
        if o[r] < 2:
            x[r, :, 15] = 0
            u[r, :, ::16] = s * (0.9 + 0.1 * rng.random((128, 8, 4))) * 2.0 ** 30
            v[r] = rng.choice([-1.0, 1.0], (128, 512)) * (0.9 + 0.1 * rng.random((128, 512))) * 2.0 ** 30
        if o[r] == 2:
            u[r, :, ::16] = s * (1.0 + 0.125 * rng.integers(0, 8, (128, 8, 4))) * 2.0 ** -30
            v[r] = rng.choice([-1.0, 1.0], (128, 512)) * (1.0 + 0.125 * rng.integers(0, 8, (128, 512))) * 2.0 ** -30
        if o[r] == 3: u[r, :, ::16] *= np.abs(s).astype(np.float32)
        k = np.full(128, [-0.125, -0.125, 0.25, 2.0 ** -8][o[r]])
        if o[r] >= 2: k[15::16] = 2.0 ** 8
        for b in range(4): w[r, i, b, i, b] = k
    c, a, m = orders(rng), orders(rng), mates(rng)
    j = np.arange(C)
    c[e == 0], m[e == 0] = j, j ^ 1
    c[e == 1], m[e == 1] = C - 1 - j, C - 1 - j
    c[e == 2], a[e == 2], m[e == 2] = C - 1 - j, j, (j + C // 2) % C
    return {"x": x.astype(np.float32).reshape(N, 128, 4 * C).astype(BF), "u": u.reshape(N, 128, 512).astype(BF), "v": v.astype(BF), **stored(c, a, m), **weights(rng, w.astype(BF))}
def setup_inputs_spread(rng):
    d = setup_inputs(rng)
    d["x"] = wide(rng, N, 128, 4 * C, cols=6)
    return d
def check_inputs(d):
    b = []
    for k in ("x", "u", "v"):
        a = np.abs(d[k].astype(np.float32))
        if not (np.isfinite(a).all() and ((a == 0) | (a >= 2.0 ** -30) & (a <= 2.0 ** 30)).all()): b.append("a value of " + k)
    j = np.arange(C)
    for k in ("cl", "pl", "ml"):
        for r in range(N):
            e = gentries(d[k][r])
            if not (np.sort(e, axis=1) == j).all(): b.append("a list of " + k)
            elif k == "ml" and ((at(e, e) != j) | (e == j)).any(): b.append("ml: mates")
    none, least, most = [emit(mx_ref.quantize(np.full((128, 16), k, np.float32).astype(BF)))[1][0, 0] for k in (0.0, 2.0 ** -8, 2.0 ** 8)]
    for r in range(N):
        if ((d["wc"][r] == 0x7F) | (d["wc"][r] == 0xFF)).any(): b.append("wc: a code that is no number")
        s = mx_ref.live(d["ws"][r])
        if ((s != none) & ((s < least) | (s > most))).any(): b.append("ws: a scale out of range")
        if (((d["wc"][r].reshape(16, 8, 512, 4) & 0x7F) != 0) & (s == none)[:, None, :, None]).any(): b.append("wc: a code other than zero under the scale of zeros")
    return b
def at(a, e):
    return np.take_along_axis(a, e, axis=1)
def above(s, a, b):
    return (at(s, a) > at(s, b)) | (at(s, a) == at(s, b)) & (a < b)
def reference(x, u, v, cl, pl, ml, wc, ws):
    qu = [mx_ref.quantize(u[r]) for r in range(N)]
    lay = [pk(wc[r], ws[r]) for r in range(N)]
    child, parent, mate = [gentries(cl[r]) for r in range(N)], [gentries(pl[r]) for r in range(N)], [gentries(ml[r]) for r in range(N)]
    j = np.tile(np.arange(C), (8, 1))
    now = [x[r] for r in range(N)]
    for step in STEP:
        t, z = [], []
        for r in range(N):
            q = mx_ref.quantize(now[r])
            s = mx_ref.matmul(qu[r], q)[::16] + np.float32(0.0)
            c, m = child[r], mate[r]
            o = np.where(above(s, j, m) == above(s, c, at(c, m)), c, at(c, m))
            new = np.argsort(o, axis=1)
            k = at(o, at(np.argsort(parent[r], axis=1), at(m, at(parent[r], new))))
            t.append(decode(q))
            p = t[r].astype(BF)
            z.append(mx_ref.quantize(((gcols(p, new).astype(np.float32) + gcols(p, k).astype(np.float32)) * np.float32(0.5)).astype(BF)))
            parent[r], mate[r] = new, k
        for r in range(N):
            h = [mx_ref.matmul(pick(lay[r], np.arange(128 * b, 128 * b + 128)), z[(r - step) % N]) * np.float32(0.03125) for b in range(4)]
            now[r] = tile([t[r][:, b::4] + gpick(h[b], parent[r]) for b in range(4)])
    y, co = np.zeros((N, 128, C), np.float32), np.zeros((N, 8, C), np.float32)
    oc, osc = np.zeros((N, 128, 4 * C), np.uint8), np.zeros((N, 16, C), np.uint8)
    for r in range(N):
        q = mx_ref.quantize(now[r])
        y[r] = mx_ref.matmul(mx_ref.quantize(v[r]), q)
        co[r] = mate[r]
        oc[r], osc[r] = emit(q)
    return {"y": y, "co": co, "oc": oc, "osc": osc}

@@ -1,0 +1,296 @@
+from concourse.bass import DstId, RemoteDMATransfer
+from concourse.mybir import dt, AluOpType as Op, ActivationFunctionType as Fn
+
+C = 320
+STEP = [1, 2, 4]
+ROUNDS = 3
+HZ = 192
+
+SCRATCH = {
+    "idf": ("sbuf", [128, C], "float32"), "idb": ("sbuf", [128, C], "bfloat16"), "id512": ("sbuf", [128, C], "float32"),
+    "t16": ("sbuf", [128, 2 * C], "bfloat16"), "pcol": ("sbuf", [128, 1], "int32"), "qi": ("sbuf", [128, 1], "int32"),
+    "qf": ("sbuf", [128, 1], "float32"), "c16": ("sbuf", [128, 20], "float32"), "pk": ("sbuf", [128, 8], "int32"),
+    "pku": ("sbuf", [128, 8], "uint16"), "mask": ("sbuf", [128, C], "bfloat16"), "keep": ("sbuf", [128, C], "bfloat16"),
+    "wts": ("sbuf", [128, 2 * C], "bfloat16"), "fours": ("sbuf", [128, 16], "bfloat16"), "dia": ("sbuf", [128, 16], "bfloat16"),
+    "thr": ("sbuf", [128, 16], "float32"), "ein": ("sbuf", [128, 516], "bfloat16"),
+    "eq": ("sbuf", [128, 512], "float8_e4m3fn_x4"), "es": ("sbuf", [128, 512], "uint8"),
+    "xin": ("sbuf", [128, 4 * C], "bfloat16"), "uin": ("sbuf", [128, 512], "bfloat16"), "vin": ("sbuf", [128, 512], "bfloat16"),
+    "ci32": ("sbuf", [128, 20], "int32"), "mi32": ("sbuf", [128, 20], "int32"), "pi32": ("sbuf", [128, 20], "int32"),
+    "cu": ("sbuf", [128, 20], "uint16"), "mu": ("sbuf", [128, 20], "uint16"), "pu": ("sbuf", [128, 20], "uint16"),
+    "wq": ("sbuf", [128, 512], "float8_e4m3fn_x4"), "wsc": ("sbuf", [128, 512], "uint8"),
+    "uq": ("sbuf", [128, 128], "float8_e4m3fn_x4"), "us": ("sbuf", [128, 128], "uint8"),
+    "uq2": ("sbuf", [128, 128], "float8_e4m3fn_x4"), "us2": ("sbuf", [128, 128], "uint8"),
+    "vq": ("sbuf", [128, 128], "float8_e4m3fn_x4"), "vs": ("sbuf", [128, 128], "uint8"),
+    "cir": ("sbuf", [128, C], "bfloat16"), "cim": ("sbuf", [128, C], "bfloat16"), "ciz": ("sbuf", [128, C], "bfloat16"),
+    "ciu": ("sbuf", [128, 20], "uint16"), "jc": ("sbuf", [128, 40], "float32"), "crep": ("sbuf", [128, C], "bfloat16"),
+    "w0": ("sbuf", [128, C], "float32"), "ca": ("sbuf", [128, C], "bfloat16"), "cam": ("sbuf", [128, C], "bfloat16"),
+    "kco": ("sbuf", [128, C], "float32"), "yt": ("sbuf", [128, C], "float32"), "tr": ("sbuf", [128, 4 * C], "bfloat16"),
+    "psa": ("psum", [128, 2048], "float32"), "psb": ("psum", [128, 2048], "float32"),
+}
+for _r in range(ROUNDS + 1):
+    SCRATCH["xq%d" % _r] = ("sbuf", [128, C], "float8_e4m3fn_x4")
+    SCRATCH["xs%d" % _r] = ("sbuf", [128, C], "uint8")
+for _r in range(ROUNDS):
+    for _n, _w, _d in (("lq", C, "float8_e4m3fn_x4"), ("ls", C, "uint8"), ("ll", 40, "uint16"), ("li", 40, "uint16"),
+                       ("zq", C, "float8_e4m3fn_x4"), ("zs", C, "uint8"), ("lst", 80, "uint16"), ("qu", 20, "uint16"),
+                       ("mg", 60, "int32"), ("sm", 512, "float32"), ("sc", C, "float32"), ("ga", C, "float32"),
+                       ("gb", C, "float32"), ("bits", 2 * C, "bfloat16"), ("zz", 2 * C, "bfloat16"), ("tb", 4 * C, "bfloat16"),
+                       ("bg", 2 * C, "float32")):
+        SCRATCH["%s%d" % (_n, _r)] = ("sbuf", [128, _w], _d)
+for _n, _d in (("tp", "float32"), ("tq", "bfloat16"), ("vp", "float32"), ("rp", "float32"), ("zt", "bfloat16"), ("xt", "bfloat16")):
+    SCRATCH[_n] = ("sbuf", [128, 4 * C], _d)
+
+LOADS = ["x", "u", "v", "cl", "pl", "ml", "wc", "ws"]
+SEMAPHORES = ["V", "A", "P", "G", "sent", "ost"] + ["d" + k for k in LOADS] + ["arr%d" % r for r in range(ROUNDS)] + ["arl%d" % r for r in range(ROUNDS)]
+
+
+def rank_program(g, core, T, topo):
+    rank = T.rank_of(core)
+    if rank is None:
+        return
+    queues = {"V": g.vector, "A": g.scalar, "P": g.tensor, "G": g, "S": g.sync}
+    count = {k: 0 for k in queues}
+    seen = {k: {} for k in queues}
+    known = {}
+
+    def need(q, deps):
+        for sem, val in sorted(set(deps), key=lambda t: -t[1]):
+            if seen[q].get(sem, 0) >= val:
+                continue
+            queues[q].wait_ge(T.sem[sem], val)
+            seen[q][sem] = val
+            for s2, v2 in known.get((sem, val), {}).items():
+                if seen[q].get(s2, 0) < v2:
+                    seen[q][s2] = v2
+
+    def run(q, deps, call, *args, **kw):
+        need(q, deps)
+        call(*args, **kw).then_inc(T.sem[q], 1)
+        count[q] += 1
+        known[(q, count[q])] = dict(seen[q])
+        return (q, count[q])
+
+    def V(call, deps, *args):
+        return run("V", deps, call, *args)
+
+    def vcp(out, in_, *deps): return run("V", deps, g.vector.tensor_copy, out, in_)
+    def vtt(out, a, b, op, *deps): return run("V", deps, g.vector.tensor_tensor, out, a, b, op)
+    def vts(out, a, s, op, *deps): return run("V", deps, g.vector.tensor_scalar, out, a, s, None, op)
+    def vts2(out, a, s, op, s2, op2, *deps): return run("V", deps, g.vector.tensor_scalar, out, a, s, s2, op, op2)
+    def vscan(out, w, x, *deps): return run("V", deps, g.vector.tensor_tensor_scan, out, w, x, 0.0, Op.mult, Op.add)
+    def vq(out, sc, x, *deps): return run("V", deps, g.vector.quantize_mx, out, sc, x)
+    def acp(out, in_, *deps, scale=1.0): return run("A", deps, g.scalar.activation, out, in_, Fn.Copy, scale=scale) if scale != 1.0 else run("A", deps, g.scalar.activation, out, in_, Fn.Copy)
+    def mm(out, w, ws, x, xs, *deps): return run("P", deps, g.tensor.matmul_mx, out, w, ws, x, xs, True, True)
+
+    def load(queue, name, out, in_):
+        queue.dma_start(out, in_).then_inc(T.sem["d" + name], 16)
+        return ("d" + name, 16)
+
+    def B(name, r): return T["%s%d" % (name, r)]
+
+    dc = load(g.scalar, "cl", T.ci32[:], T.cl[:])
+    dm = load(g.scalar, "ml", T.mi32[:], T.ml[:])
+    dp = load(g.scalar, "pl", T.pi32[:], T.pl[:])
+    dx = load(g.sync, "x", T.xin[:], T.x[:])
+    du = load(g.sync, "u", T.uin[:], T.u[:])
+    dwc = load(g.sync, "wc", T.wq[:].bitcast(dt.uint8), T.wc[:])
+    dws = load(g.sync, "ws", T.wsc[:], T.ws[:])
+    dv = load(g.sync, "v", T.vin[:], T.v[:])
+
+    on = V(g.vector.memset, (), T.ein[:], 1.0)
+    fo = V(g.vector.memset, (), T.fours[:], 4.0)
+
+    def iota(buf, pattern, base, cm, flag):
+        if flag:
+            return run("G", (), g.iota, buf[:], pattern, base, cm, allow_small_or_imprecise_dtypes=True)
+        return run("G", (), g.iota, buf[:], pattern, base, cm)
+    i_p = iota(T.pcol, [[0, 1]], 0, 1, False)
+    i_c = iota(T.c16, [[16, 20]], 0, 0, True)
+    i_b = iota(T.idb, [[1, C]], -160, 0, True)
+    i_t = iota(T.t16, [[0, 40], [1, 16]], 0, 0, True)
+    i_f = iota(T.idf, [[1, C]], 0, 0, True)
+    i_5 = iota(T.id512, [[512, C]], 0, 0, True)
+    i_k = iota(T.pk, [[16, 8]], 0, 0, False)
+    i_e = run("G", [on], g.affine_select, T.ein[:], T.ein[:], [[1, 516]], Op.is_equal, 0.0, -3, -4)
+
+    t = vts(T.qi[:], T.pcol[:], 15, Op.bitwise_and, i_p)
+    tqf = vcp(T.qf[:], T.qi[:], t)
+    tj = vts(T.jc[:, 0:20], T.c16[:], T.qf[:, 0:1], Op.add, i_c, tqf)
+    tcu = vcp(T.cu[:], T.ci32[:], dc)
+    tmu = vcp(T.mu[:], T.mi32[:], dm)
+    tpu = vcp(T.pu[:], T.pi32[:], dp)
+    tcir = vcp(T.cir[:, 0:C].indirect(T.cu[:, 0:20]), T.idb[:], i_b, tcu)
+    tcrep = acp(T.crep[:], T.idb[:, 0:C].indirect(T.cu[:, 0:20]), i_b, tcu)
+    tmask = vts(T.mask[:], T.t16[:, 0:C], T.qf[:, 0:1], Op.is_equal, i_t, tqf)
+    tkeep = vts(T.keep[:], T.t16[:, 0:C], 0.0, Op.not_equal, i_t)
+    tcim = vtt(T.cim[:], T.cir[:], T.mask[:], Op.mult, tcir, tmask)
+    tciz = vscan(T.ciz[:], T.keep[:], T.cim[:], tkeep, tcim)
+    tciu = vts(T.ciu[:], T.ciz[:, 15:C:16], 160.0, Op.add, tciz)
+    tci = vts(T.jc[:, 20:40], T.ciz[:, 15:C:16], 160.0, Op.add, tciz)
+    tjc = max(tj, tci)
+    tw0 = vtt(T.w0[:], T.id512[:, 0:C].indirect(T.cu[:, 0:20]), T.idf[:], Op.add, i_5, i_f, tcu)
+    tr2 = acp(T.gb0[:], T.w0[:, 0:C].indirect(T.mu[:, 0:20]), tw0, tmu)
+    HX = C // 2
+    tx = [vq(T.xq0[:, h:h + HX], T.xs0[:, h:h + HX], T.xin[:, 4 * h:4 * (h + HX)], dx) for h in (0, HX)]
+    tpk = vcp(T.pku[:], T.pk[:], i_k)
+    tuq = vq(T.uq[:], T.us[:], T.uin[:], du)
+    tu1 = vcp(T.uq2[:, 0:128].bitcast(dt.uint32), T.uq[:, 0:128].bitcast(dt.uint32).indirect(T.pku[:, 0:8]), tuq, tpk)
+    tu2 = vcp(T.us2[:, 0:128], T.us[:, 0:128].indirect(T.pku[:, 0:8]), tuq, tpk)
+    te = [vq(T.eq[:, 128 * b:128 * b + 128], T.es[:, 128 * b:128 * b + 128], T.ein[:, 3 - b:515 - b], i_e) for b in range(4)]
+
+    def statics(r, tgm):
+        bg, mg, sm, lst = B("bg", r), B("mg", r), B("sm", r), B("lst", r)
+        t1 = vscan(bg[:, C:2 * C], T.keep[:], bg[:, 0:C], tgm, tkeep)
+        t2 = vcp(mg[:, 40:60], bg[:, C + 15:2 * C:16], t1)
+        t3 = vts(mg[:, 0:20], mg[:, 40:60], 9, Op.logical_shift_right, t2)
+        t4 = vts(mg[:, 20:40], mg[:, 40:60], 511, Op.bitwise_and, t2)
+        t5 = vtt(sm[:, 0:40], T.jc[:], mg[:, 0:40], Op.min, t4, t3, tjc)
+        t6 = vtt(sm[:, 40:80], T.jc[:], mg[:, 0:40], Op.max, t4, t3, tjc)
+        t7 = vcp(lst[:], sm[:, 0:80], t5, t6)
+        t8 = vtt(sm[:, 80:120], T.jc[:], mg[:, 0:40], Op.subtract, t4)
+        t9 = vts(sm[:, 120:160], sm[:, 80:120], 0.0, Op.is_lt, t8)
+        t10 = vtt(sm[:, 160:180], sm[:, 120:140], sm[:, 140:160], Op.is_equal, t9)
+        return t7, t10, t4
+
+    tgm = vtt(T.bg0[:, 0:C], T.gb0[:, 0:C].indirect(T.ciu[:, 0:20]), T.mask[:], Op.mult, tr2, tciu, tmask)
+    tl, tsm, tmg = statics(0, tgm)
+    twt = vts2(T.wts[:], T.t16[:], T.qf[:, 0:1], Op.not_equal, 4.0, Op.mult, i_t, tqf)
+    td = vts2(T.dia[:], T.t16[:, 0:16], T.qf[:, 0:1], Op.is_equal, 0.6, Op.mult, i_t, tqf)
+    tth = vscan(T.thr[:], T.fours[:], T.dia[:], fo, td)
+    tca = vcp(T.ca[:, 0:C].indirect(T.pu[:, 0:20]), T.crep[:], tcrep, tpu)
+    tcam = acp(T.cam[:], T.ca[:, 0:C].indirect(T.mu[:, 0:20]), tca, tmu)
+
+    def makeq(r, src, off, toff, *deps):
+        tb = B("tb", r)
+        t1 = vtt(tb[:, 0:C], src[:, 0:C].indirect(off), T.mask[:], Op.mult, toff, tmask, *deps)
+        t2 = vscan(tb[:, C:2 * C], T.keep[:], tb[:, 0:C], t1, tkeep)
+        return vts(B("qu", r)[:], tb[:, C + 15:2 * C:16], 160.0, Op.add, t2)
+
+    sent = [0]
+
+    def send(dst, out, src, sem, *deps):
+        need("G", deps)
+        rid, pid, _ = topo.addr(dst)
+        m = 0
+        for e in topo.engines(core, dst)[:8]:
+            m |= 1 << e
+        g.remote_dma(out, src, T.sem[sem], T.sem.sent, pid, rid, m)
+        sent[0] += 8
+
+    tq = None
+    t_tq = []
+    t_r = [()] * 4
+    tX = []
+    t_va = []
+    for r in range(ROUNDS):
+        dst = T.cores[(rank + STEP[r]) % len(T.cores)]
+        xq, xs, lst, sm, mg = B("xq", r), B("xs", r), B("lst", r), B("sm", r), B("mg", r)
+        sc, ga, gb, bits, zz, li = B("sc", r), B("ga", r), B("gs", r), B("bits", r), B("zz", r), B("li", r)
+        send(dst, B("lq", r)[:, 0:C].bitcast(dt.uint8), xq[:, 0:C].bitcast(dt.uint8), "arr%d" % r, *tx)
+        send(dst, B("ls", r)[:, 0:C], xs[:, 0:C], "arr%d" % r, *tx)
+        ps = [mm(T.psb[:, 512 * h:512 * h + HX], T.uq2[:], T.us2[:], xq[:, HX * h:HX * h + HX], xs[:, HX * h:HX * h + HX], tx[h], tu1, tu2, *t_tq) for h in (0, 1)]
+        pt = [mm(T.psa[:, 512 * b:512 * b + C], T.eq[:, 128 * b:128 * b + 128], T.es[:, 128 * b:128 * b + 128], xq[:, 0:C], xs[:, 0:C], te[b], *tx, *t_r[b]) for b in range(4)]
+        ts0 = vcp(sc[:, 0:HX], T.psb[:, 0:HX], ps[0])
+        ts1 = acp(sc[:, HX:C], T.psb[:, 512:512 + HX], ps[1])
+        tga = acp(ga[:], sc[:, 0:C].indirect(lst[:, 20:40]), ts0, ts1, tl)
+        tgb = vcp(gb[:], sc[:, 0:C].indirect(lst[:, 0:20]), ts0, ts1, tl)
+        tb0 = vtt(bits[:, 0:C], sc[:, 0:C].indirect(lst[:, 40:60]), gb[:], Op.is_le, tgb)
+        tb1 = vtt(bits[:, C:2 * C], sc[:, 0:C].indirect(lst[:, 60:80]), ga[:], Op.is_le, tga)
+        tz = vscan(zz[:], T.wts[:], bits[:], twt, tb0, tb1)
+        e1 = vts(sm[:, 180:220], zz[:, 15:2 * C:16], T.thr[:, 15:16], Op.is_ge, tz, tth)
+        e2 = vtt(sm[:, 220:240], sm[:, 180:200], sm[:, 200:220], Op.is_equal, e1)
+        e3 = vtt(sm[:, 240:260], sm[:, 220:240], sm[:, 160:180], Op.is_equal, e2, tsm)
+        e4 = vtt(sm[:, 260:280], sm[:, 240:260], sm[:, 80:100], Op.mult, e3)
+        e5 = vtt(sm[:, 280:300], sm[:, 260:280], mg[:, 0:20], Op.add, e4)
+        phu = B("phu", r)
+        tphu = vcp(phu[:, 0:20], sm[:, 280:300], e5)
+        tt_ = [acp(T.tp[:, C * b:C * b + C], T.psa[:, 512 * b:512 * b + C], pt[b], *tX) for b in range(4)]
+        phr = B("phr", r)
+        tphr = acp(phr[:, 0:C], T.idb[:, 0:C].indirect(phu[:, 0:20]), tphu)
+        e6 = vtt(sm[:, 300:320], sm[:, 240:260], sm[:, 100:120], Op.mult, e3)
+        e7 = vtt(sm[:, 320:340], sm[:, 300:320], mg[:, 20:40], Op.add, e6)
+        tla = vcp(li[:, 0:20], sm[:, 320:340], e7)
+        if r == 0:
+            tq = makeq(0, T.cam, T.pu[:, 0:20], tpu, tcam)
+        tb = B("tb", r)
+        k1 = vtt(tb[:, 2 * C:3 * C], phr[:, 0:C].indirect(B("qu", r)[:, 0:20]), T.mask[:], Op.mult, tphr, tq)
+        k2 = vscan(tb[:, 3 * C:4 * C], T.keep[:], tb[:, 2 * C:3 * C], k1)
+        tlk = vts(li[:, 20:40], tb[:, 3 * C + 15:4 * C:16], 160.0, Op.add, k2)
+        send(dst, B("ll", r)[:], li[:], "arl%d" % r, tla, tlk)
+        if r + 1 < ROUNDS:
+            tcph = acp(phr[:, C:2 * C], T.crep[:, 0:C].indirect(phu[:, 0:20]), tphu, tcrep)
+            ta1 = acp(B("gb", r + 1)[:], T.w0[:, 0:C].indirect(li[:, 20:40]), tlk, tw0)
+            ta2 = acp(B("gb", r)[:] if r else T.kco[:], B("gb", r + 1)[:, 0:C].indirect(li[:, 0:20]), ta1, tla)
+            src = B("gb", r) if r else T.kco
+            tgm = vtt(B("bg", r + 1)[:, 0:C], src[:, 0:C].indirect(T.ciu[:, 0:20]), T.mask[:], Op.mult, ta2)
+            tl, tsm, tmg = statics(r + 1, tgm)
+            tm2 = vcp(B("phu", r + 1)[:, 20:40], B("mg", r + 1)[:, 0:20], tmg)
+        else:
+            ta1 = acp(B("gb", r)[:], T.idf[:, 0:C].indirect(li[:, 20:40]), tlk, i_f)
+            tco = acp(T.kco[:], B("gb", r)[:, 0:C].indirect(li[:, 0:20]), ta1, tla)
+            need("S", [tco])
+            g.sync.dma_start(T.co[:], T.kco[0:128:16, :]).then_inc(T.sem.ost, 16)
+        if r == 0:
+            tvq = vq(T.vq[:], T.vs[:], T.vin[:], dv)
+        arr, arl = ("arr%d" % r, 16), ("arl%d" % r, 8)
+        pq = [mm(T.psb[:, 512 * b:512 * b + C], T.eq[:, 128 * b:128 * b + 128], T.es[:, 128 * b:128 * b + 128], B("lq", r)[:], B("ls", r)[:], arr, ts0, ts1) for b in range(4)]
+        t_tq = [acp(T.tq[:, C * b:C * b + C], T.psb[:, 512 * b:512 * b + C], pq[b], *t_va, scale=0.5) for b in range(4)]
+        ll = B("ll", r)
+        tzr = t_z if r else []
+        t_cp, tv = {}, {}
+        for kind, b in ((("c", 0), ("c", 1), ("c", 2), ("c", 3), ("v", 0), ("v", 1), ("v", 2), ("v", 3)) if r == 0 else
+                        (("c", 0), ("c", 1), ("v", 0), ("c", 2), ("v", 1), ("c", 3), ("v", 2), ("v", 3))):
+            pl = slice(C * b, C * b + C)
+            if kind == "c":
+                t_cp[b] = vcp(T.tr[:, pl], T.tq[:, pl], t_tq[b])
+            else:
+                tv[b] = vtt(T.vp[:, pl], T.tq[:, pl].indirect(ll[:, 20:40]), T.tr[:, pl], Op.add, t_cp[b], arl, *tzr)
+        t_va = [tv[3]]
+        za = [acp(T.zt[:, b:4 * C:4], T.vp[:, C * b:C * b + C].indirect(ll[:, 0:20]), tv[b], arl) for b in range(3)]
+        z3 = vcp(T.zt[:, 3:4 * HZ:4], T.vp[:, 3 * C:4 * C].indirect(ll[:, 0:HZ // 16]), tv[3])
+        za.append(acp(T.zt[:, 4 * HZ + 3:4 * C:4], T.vp[:, 3 * C:4 * C].indirect(ll[:, HZ // 16:20]), tv[3]))
+        t_z = za + [z3]
+        zq, zs = B("zq", r), B("zs", r)
+        tz0 = vq(zq[:, 0:HZ], zs[:, 0:HZ], T.zt[:, 0:4 * HZ], z3, za[2])
+        tz1 = vq(zq[:, HZ:C], zs[:, HZ:C], T.zt[:, 4 * HZ:4 * C], z3, za[3])
+        last = r + 1 == ROUNDS
+        order = [3, 0, 1, 2] if last else [0, 1, 2, 3]
+        pr = {}
+        for b in order:
+            pr[b] = mm(T.psa[:, 512 * b:512 * b + C], T.wq[:, 128 * b:128 * b + 128], T.wsc[:, 128 * b:128 * b + 128], zq[:], zs[:], dwc, dws, tz0, tz1, tt_[b])
+        if not last:
+            tcpm = acp(B("phr", r + 1)[:, C:2 * C] if False else B("cpm", r)[:], phr[:, C:2 * C].indirect(B("phu", r + 1)[:, 20:40]), tcph, tm2)
+        tr = {}
+        for b in order:
+            o, i = T.rp[:, C * b:C * b + C], T.psa[:, 512 * b:512 * b + C]
+            if last and b == 3:
+                tr[b] = vts(o, i, 0.03125, Op.mult, pr[b], *tX)
+            else:
+                tr[b] = acp(o, i, pr[b], *tX, scale=0.03125)
+        t_r = [[tr[b]] for b in range(4)]
+        if not last:
+            tq = makeq(r + 1, B("cpm", r), phu[:, 0:20], tphu, tcpm)
+        tX = [vtt(T.xt[:, b:4 * C:4], T.rp[:, C * b:C * b + C].indirect(li[:, 0:20]), T.tp[:, C * b:C * b + C], Op.add, tr[b], tt_[b], tla) for b in order]
+        nq, ns = B("xq", r + 1), B("xs", r + 1)
+        tx = [vq(nq[:, h:h + HX], ns[:, h:h + HX], T.xt[:, 4 * h:4 * (h + HX)], *tX) for h in (0, HX)]
+
+    need("S", tx)
+    g.sync.dma_start(T.oc[:, 0:4 * C], T.xq3[:, 0:C].bitcast(dt.uint8)).then_inc(T.sem.ost, 16)
+    for k in range(4):
+        g.sync.dma_start(T.osc[4 * k:4 * k + 4, 0:C], T.xs3[32 * k:32 * k + 4, 0:C]).then_inc(T.sem.ost, 16)
+    py = [mm(T.psb[:, 512 * h:512 * h + HX], T.vq[:], T.vs[:], T.xq3[:, HX * h:HX * h + HX], T.xs3[:, HX * h:HX * h + HX], tx[h], tvq, *t_tq) for h in (0, 1)]
+    ty0 = vcp(T.yt[:, 0:HX], T.psb[:, 0:HX], py[0])
+    ty1 = acp(T.yt[:, HX:C], T.psb[:, 512:512 + HX], py[1])
+    need("A", [ty0, ty1])
+    g.scalar.dma_start(T.y[:], T.yt[:]).then_inc(T.sem.ost, 16)
+    need("G", [(q, count[q]) for q in ("V", "A", "P", "G")])
+    g.wait_ge(T.sem.ost, 16 * 7)
+    g.wait_ge(T.sem.sent, sent[0])
+
+
+for _r in range(ROUNDS):
+    SCRATCH["gs%d" % _r] = ("sbuf", [128, C], "float32")
+    SCRATCH["phr%d" % _r] = ("sbuf", [128, 2 * C], "bfloat16")
+    SCRATCH["phu%d" % _r] = ("sbuf", [128, 40], "uint16")
+    if _r < ROUNDS - 1:
+        SCRATCH["cpm%d" % _r] = ("sbuf", [128, C], "bfloat16")

@@ -2,46 +2,38 @@ from concourse.bass import DstId, RemoteDMATransfer
 from concourse.mybir import dt, AluOpType as Op, ActivationFunctionType as Fn
 
 C = 320
+H = C // 2
 STEP = [1, 2, 4]
 ROUNDS = 3
 HZ = 192
+X4, F32, B16, I32, U16, U8 = "float8_e4m3fn_x4", "float32", "bfloat16", "int32", "uint16", "uint8"
 
-SCRATCH = {
-    "idf": ("sbuf", [128, C], "float32"), "idb": ("sbuf", [128, C], "bfloat16"), "id512": ("sbuf", [128, C], "float32"),
-    "t16": ("sbuf", [128, 2 * C], "bfloat16"), "pcol": ("sbuf", [128, 1], "int32"), "qi": ("sbuf", [128, 1], "int32"),
-    "qf": ("sbuf", [128, 1], "float32"), "c16": ("sbuf", [128, 20], "float32"), "pk": ("sbuf", [128, 8], "int32"),
-    "pku": ("sbuf", [128, 8], "uint16"), "mask": ("sbuf", [128, C], "bfloat16"), "keep": ("sbuf", [128, C], "bfloat16"),
-    "wts": ("sbuf", [128, 2 * C], "bfloat16"), "fours": ("sbuf", [128, 16], "bfloat16"), "dia": ("sbuf", [128, 16], "bfloat16"),
-    "thr": ("sbuf", [128, 16], "float32"), "ein": ("sbuf", [128, 516], "bfloat16"),
-    "eq": ("sbuf", [128, 512], "float8_e4m3fn_x4"), "es": ("sbuf", [128, 512], "uint8"),
-    "xin": ("sbuf", [128, 4 * C], "bfloat16"), "uin": ("sbuf", [128, 512], "bfloat16"), "vin": ("sbuf", [128, 512], "bfloat16"),
-    "ci32": ("sbuf", [128, 20], "int32"), "mi32": ("sbuf", [128, 20], "int32"), "pi32": ("sbuf", [128, 20], "int32"),
-    "cu": ("sbuf", [128, 20], "uint16"), "mu": ("sbuf", [128, 20], "uint16"), "pu": ("sbuf", [128, 20], "uint16"),
-    "wq": ("sbuf", [128, 512], "float8_e4m3fn_x4"), "wsc": ("sbuf", [128, 512], "uint8"),
-    "uq": ("sbuf", [128, 128], "float8_e4m3fn_x4"), "us": ("sbuf", [128, 128], "uint8"),
-    "uq2": ("sbuf", [128, 128], "float8_e4m3fn_x4"), "us2": ("sbuf", [128, 128], "uint8"),
-    "vq": ("sbuf", [128, 128], "float8_e4m3fn_x4"), "vs": ("sbuf", [128, 128], "uint8"),
-    "cir": ("sbuf", [128, C], "bfloat16"), "cim": ("sbuf", [128, C], "bfloat16"), "ciz": ("sbuf", [128, C], "bfloat16"),
-    "ciu": ("sbuf", [128, 20], "uint16"), "jc": ("sbuf", [128, 40], "float32"), "crep": ("sbuf", [128, C], "bfloat16"),
-    "w0": ("sbuf", [128, C], "float32"), "ca": ("sbuf", [128, C], "bfloat16"), "cam": ("sbuf", [128, C], "bfloat16"),
-    "kco": ("sbuf", [128, C], "float32"), "yt": ("sbuf", [128, C], "float32"), "tr": ("sbuf", [128, 4 * C], "bfloat16"),
-    "psa": ("psum", [128, 2048], "float32"), "psb": ("psum", [128, 2048], "float32"),
-}
+SCRATCH = {}
+for _names, _w, _d in (
+        ("idf id512", C, F32), ("idb mask keep t16", C, B16), ("wts", 2 * C, B16), ("pcol qi", 1, I32), ("qf", 1, F32),
+        ("c16", 20, F32), ("pk", 8, I32), ("pku", 8, U16), ("fours dia", 16, B16), ("thr", 16, F32), ("ein", 516, B16),
+        ("eq", 512, X4), ("es", 512, U8),
+        ("xin", 4 * C, B16), ("uin vin", 512, B16), ("ci32 mi32 pi32", 20, I32), ("cu mu pu", 20, U16),
+        ("wq", 512, X4), ("wsc", 512, U8), ("uq uq2 vq", 128, X4), ("us us2 vs", 128, U8),
+        ("cir cim ciz crep", C, B16), ("ciu ap thu m2u", 20, U16), ("jc jc0", 40, F32), ("w0 an am pp pir tpr", C, F32),
+        ("sc ga gb f0 f1 kco yt rg", C, F32), ("bits zz", 2 * C, B16), ("lst", 80, U16), ("sm", 340, F32), ("mg", 120, I32),
+        ("bg kg", 2 * C, F32), ("ph", 4 * C, B16), ("tb", 4 * C, B16),
+        ("tp vp rp", 4 * C, F32), ("tq tk zt xt", 4 * C, B16), ("zq", C, X4), ("zs", C, U8)):
+    for _n in _names.split():
+        SCRATCH[_n] = ("sbuf", [128, _w], _d)
 for _r in range(ROUNDS + 1):
-    SCRATCH["xq%d" % _r] = ("sbuf", [128, C], "float8_e4m3fn_x4")
-    SCRATCH["xs%d" % _r] = ("sbuf", [128, C], "uint8")
+    SCRATCH["xq%d" % _r] = ("sbuf", [128, C], X4)
+    SCRATCH["xs%d" % _r] = ("sbuf", [128, C], U8)
 for _r in range(ROUNDS):
-    for _n, _w, _d in (("lq", C, "float8_e4m3fn_x4"), ("ls", C, "uint8"), ("ll", 40, "uint16"), ("li", 40, "uint16"),
-                       ("zq", C, "float8_e4m3fn_x4"), ("zs", C, "uint8"), ("lst", 80, "uint16"), ("qu", 20, "uint16"),
-                       ("mg", 60, "int32"), ("sm", 512, "float32"), ("sc", C, "float32"), ("ga", C, "float32"),
-                       ("gb", C, "float32"), ("bits", 2 * C, "bfloat16"), ("zz", 2 * C, "bfloat16"), ("tb", 4 * C, "bfloat16"),
-                       ("bg", 2 * C, "float32")):
-        SCRATCH["%s%d" % (_n, _r)] = ("sbuf", [128, _w], _d)
-for _n, _d in (("tp", "float32"), ("tq", "bfloat16"), ("vp", "float32"), ("rp", "float32"), ("zt", "bfloat16"), ("xt", "bfloat16")):
-    SCRATCH[_n] = ("sbuf", [128, 4 * C], _d)
+    SCRATCH["lq%d" % _r] = ("sbuf", [128, C], X4)
+    SCRATCH["ls%d" % _r] = ("sbuf", [128, C], U8)
+    for _n in ("lk", "lv", "lz", "kp", "vl", "zl"):
+        SCRATCH["%s%d" % (_n, _r)] = ("sbuf", [128, 20], U16)
+SCRATCH["psa"] = ("psum", [128, 2048], F32)
+SCRATCH["psb"] = ("psum", [128, 2048], F32)
 
 LOADS = ["x", "u", "v", "cl", "pl", "ml", "wc", "ws"]
-SEMAPHORES = ["V", "A", "P", "G", "sent", "ost"] + ["d" + k for k in LOADS] + ["arr%d" % r for r in range(ROUNDS)] + ["arl%d" % r for r in range(ROUNDS)]
+SEMAPHORES = ["V", "A", "P", "G", "sent", "ost"] + ["d" + k for k in LOADS] + ["%s%d" % (k, r) for k in ("arq", "ark", "arv", "arz") for r in range(ROUNDS)]
 
 
 def rank_program(g, core, T, topo):
@@ -70,23 +62,42 @@ def rank_program(g, core, T, topo):
         known[(q, count[q])] = dict(seen[q])
         return (q, count[q])
 
-    def V(call, deps, *args):
-        return run("V", deps, call, *args)
-
+    def vfill(ap, k): return run("V", (), g.vector.memset, ap, k)
     def vcp(out, in_, *deps): return run("V", deps, g.vector.tensor_copy, out, in_)
     def vtt(out, a, b, op, *deps): return run("V", deps, g.vector.tensor_tensor, out, a, b, op)
     def vts(out, a, s, op, *deps): return run("V", deps, g.vector.tensor_scalar, out, a, s, None, op)
     def vts2(out, a, s, op, s2, op2, *deps): return run("V", deps, g.vector.tensor_scalar, out, a, s, s2, op, op2)
     def vscan(out, w, x, *deps): return run("V", deps, g.vector.tensor_tensor_scan, out, w, x, 0.0, Op.mult, Op.add)
-    def vq(out, sc, x, *deps): return run("V", deps, g.vector.quantize_mx, out, sc, x)
-    def acp(out, in_, *deps, scale=1.0): return run("A", deps, g.scalar.activation, out, in_, Fn.Copy, scale=scale) if scale != 1.0 else run("A", deps, g.scalar.activation, out, in_, Fn.Copy)
+    def vqt(out, sc, x, *deps): return run("V", deps, g.vector.quantize_mx, out, sc, x)
+    def acp(out, in_, *deps): return run("A", deps, g.scalar.activation, out, in_, Fn.Copy)
+    def asc(out, in_, k, *deps): return run("A", deps, g.scalar.activation, out, in_, Fn.Copy, scale=k)
     def mm(out, w, ws, x, xs, *deps): return run("P", deps, g.tensor.matmul_mx, out, w, ws, x, xs, True, True)
 
     def load(queue, name, out, in_):
         queue.dma_start(out, in_).then_inc(T.sem["d" + name], 16)
         return ("d" + name, 16)
 
-    def B(name, r): return T["%s%d" % (name, r)]
+    def R(name, r): return T["%s%d" % (name, r)]
+    def pl(b): return slice(C * b, C * b + C)
+    def bank(ps, b): return ps[:, 512 * b:512 * b + C]
+    def w128(b): return slice(128 * b, 128 * b + 128)
+    def gat(t, lst): return t[:, 0:C].indirect(lst[:, 0:20])
+
+    sent = [0]
+
+    def send(r, out, src, sem, *deps):
+        need("G", deps)
+        dst = T.cores[(rank + STEP[r]) % len(T.cores)]
+        rid, pid, _ = topo.addr(dst)
+        eng = topo.engines(core, dst)[:8]
+        g.remote_dma(out, src, T.sem[sem], T.sem.sent, pid, rid, sum(1 << e for e in eng))
+        sent[0] += len(eng)
+
+    later = []
+
+    def fill(n=99):
+        for _ in range(min(n, len(later))):
+            later.pop(0)()
 
     dc = load(g.scalar, "cl", T.ci32[:], T.cl[:])
     dm = load(g.scalar, "ml", T.mi32[:], T.ml[:])
@@ -97,200 +108,280 @@ def rank_program(g, core, T, topo):
     dws = load(g.sync, "ws", T.wsc[:], T.ws[:])
     dv = load(g.sync, "v", T.vin[:], T.v[:])
 
-    on = V(g.vector.memset, (), T.ein[:], 1.0)
-    fo = V(g.vector.memset, (), T.fours[:], 4.0)
-
-    def iota(buf, pattern, base, cm, flag):
-        if flag:
-            return run("G", (), g.iota, buf[:], pattern, base, cm, allow_small_or_imprecise_dtypes=True)
-        return run("G", (), g.iota, buf[:], pattern, base, cm)
+    def iota(buf, pattern, base, cm, flag=True):
+        kw = {"allow_small_or_imprecise_dtypes": True} if flag else {}
+        return run("G", (), g.iota, buf[:], pattern, base, cm, **kw)
     i_p = iota(T.pcol, [[0, 1]], 0, 1, False)
-    i_c = iota(T.c16, [[16, 20]], 0, 0, True)
-    i_b = iota(T.idb, [[1, C]], -160, 0, True)
-    i_t = iota(T.t16, [[0, 40], [1, 16]], 0, 0, True)
-    i_f = iota(T.idf, [[1, C]], 0, 0, True)
-    i_5 = iota(T.id512, [[512, C]], 0, 0, True)
+    i_c = iota(T.c16, [[16, 20]], 0, 0)
+    i_t = iota(T.t16, [[0, 20], [1, 16]], 0, 0)
+    i_b = iota(T.idb, [[1, C]], -160, 0)
+    i_5 = iota(T.id512, [[512, C]], 0, 0)
     i_k = iota(T.pk, [[16, 8]], 0, 0, False)
-    i_e = run("G", [on], g.affine_select, T.ein[:], T.ein[:], [[1, 516]], Op.is_equal, 0.0, -3, -4)
+    t_e1 = vfill(T.ein[:], 1.0)
+    t_fo = vfill(T.fours[:], 4.0)
+    i_e = run("G", [t_e1], g.affine_select, T.ein[:], T.ein[:], [[1, 516]], Op.is_equal, 0.0, -3, -4)
+    i_f = iota(T.idf, [[1, C]], 0, 0)
 
-    t = vts(T.qi[:], T.pcol[:], 15, Op.bitwise_and, i_p)
-    tqf = vcp(T.qf[:], T.qi[:], t)
+    tqi = vts(T.qi[:], T.pcol[:], 15, Op.bitwise_and, i_p)
+    tqf = vcp(T.qf[:], T.qi[:], tqi)
     tj = vts(T.jc[:, 0:20], T.c16[:], T.qf[:, 0:1], Op.add, i_c, tqf)
+    tj0 = vts(T.jc0[:, 20:40], T.c16[:], T.qf[:, 0:1], Op.add, i_c, tqf)
+    tmask = vts(T.mask[:], T.t16[:], T.qf[:, 0:1], Op.is_equal, i_t, tqf)
+    tkeep = vts(T.keep[:], T.t16[:], 0.0, Op.not_equal, i_t)
+    twt = [vts2(T.wts[:, h:h + C], T.t16[:], T.qf[:, 0:1], Op.not_equal, 4.0, Op.mult, i_t, tqf) for h in (0, C)]
+    tdi = vts2(T.dia[:], T.t16[:, 0:16], T.qf[:, 0:1], Op.is_equal, 0.6, Op.mult, i_t, tqf)
+    tth = vscan(T.thr[:], T.fours[:], T.dia[:], t_fo, tdi)
     tcu = vcp(T.cu[:], T.ci32[:], dc)
+    tj1 = vcp(T.jc0[:, 0:20], T.ci32[:], dc)
     tmu = vcp(T.mu[:], T.mi32[:], dm)
+    tg0 = vcp(T.mg[:, 20:40], T.mi32[:], dm)
+    tcrep = acp(T.crep[:], gat(T.idb, T.cu), i_b, tcu)
+
+    def wrap16(src, off, out, col, *deps):
+        s = {}
+        def a(): s[1] = vtt(T.tb[:, col:col + C], src.indirect(off), T.mask[:], Op.mult, tmask, *deps)
+        def b(): s[2] = vscan(T.tb[:, col + C:col + 2 * C], T.keep[:], T.tb[:, col:col + C], s[1], tkeep)
+        def c(): s[3] = vts(out, T.tb[:, col + C + 15:col + 2 * C:16], 160.0, Op.add, s[2])
+        return s, a, b, c
+
+    st = {}
+
+    def rest(jc, tjc, tmg):
+        mg, sm = T.mg, T.sm
+        def s5(): st[5] = vtt(sm[:, 0:40], jc[:], mg[:, 0:40], Op.min, *tmg(), *tjc())
+        def s6(): st[6] = vtt(sm[:, 40:80], jc[:], mg[:, 0:40], Op.max, *tmg(), *tjc())
+        def s7(): st["l"] = vcp(T.lst[:], sm[:, 0:80], st[5], st[6])
+        def s8(): st["d"] = vtt(sm[:, 80:120], jc[:], mg[:, 0:40], Op.subtract, *tmg(), *tjc())
+        def s9(): st[9] = vts(sm[:, 120:160], sm[:, 80:120], 0.0, Op.is_lt, st["d"])
+        def s10(): st["q"] = vtt(sm[:, 160:180], sm[:, 120:140], sm[:, 140:160], Op.is_equal, st[9])
+        return [s5, s6, s8, s7, s9, s10]
+
+    te, tci = [], {}
+
+    def unpacker(b):
+        te.append(vqt(T.eq[:, w128(b)], T.es[:, w128(b)], T.ein[:, 3 - b:515 - b], i_e))
+
+    def inverse():
+        s = {}
+        def o(): s[0] = vcp(T.cir[:, 0:C].indirect(T.cu[:, 0:20]), T.idb[:], i_b, tcu)
+        def a(): s[1] = vtt(T.cim[:], T.cir[:], T.mask[:], Op.mult, s[0], tmask)
+        def b(): s[2] = vscan(T.ciz[:], T.keep[:], T.cim[:], s[1], tkeep)
+        def c(): tci["u"] = vts(T.ciu[:], T.ciz[:, 15:C:16], 160.0, Op.add, s[2])
+        def d(): tci["f"] = vts(T.jc[:, 20:40], T.ciz[:, 15:C:16], 160.0, Op.add, s[2])
+        return [o, a, b, c, d]
+
     tpu = vcp(T.pu[:], T.pi32[:], dp)
-    tcir = vcp(T.cir[:, 0:C].indirect(T.cu[:, 0:20]), T.idb[:], i_b, tcu)
-    tcrep = acp(T.crep[:], T.idb[:, 0:C].indirect(T.cu[:, 0:20]), i_b, tcu)
-    tmask = vts(T.mask[:], T.t16[:, 0:C], T.qf[:, 0:1], Op.is_equal, i_t, tqf)
-    tkeep = vts(T.keep[:], T.t16[:, 0:C], 0.0, Op.not_equal, i_t)
-    tcim = vtt(T.cim[:], T.cir[:], T.mask[:], Op.mult, tcir, tmask)
-    tciz = vscan(T.ciz[:], T.keep[:], T.cim[:], tkeep, tcim)
-    tciu = vts(T.ciu[:], T.ciz[:, 15:C:16], 160.0, Op.add, tciz)
-    tci = vts(T.jc[:, 20:40], T.ciz[:, 15:C:16], 160.0, Op.add, tciz)
-    tjc = max(tj, tci)
-    tw0 = vtt(T.w0[:], T.id512[:, 0:C].indirect(T.cu[:, 0:20]), T.idf[:], Op.add, i_5, i_f, tcu)
-    tr2 = acp(T.gb0[:], T.w0[:, 0:C].indirect(T.mu[:, 0:20]), tw0, tmu)
-    HX = C // 2
-    tx = [vq(T.xq0[:, h:h + HX], T.xs0[:, h:h + HX], T.xin[:, 4 * h:4 * (h + HX)], dx) for h in (0, HX)]
+    s, a, b, c = wrap16(T.crep[:, 0:C], T.mu[:, 0:20], T.mg[:, 0:20], 0, tcrep, tmu)
+    a()
+    tan = vcp(T.an[:, 0:C].indirect(T.pu[:, 0:20]), T.id512[:], i_5, tpu)
+    tam = acp(T.am[:], gat(T.an, T.mu), tan, tmu)
+    b()
+    tx = [vqt(T.xq0[:, 0:H], T.xs0[:, 0:H], T.xin[:, 0:2 * C], dx)]
+    c()
+    tx.append(vqt(T.xq0[:, H:C], T.xs0[:, H:C], T.xin[:, 2 * C:4 * C], dx))
+    t_cm = s[3]
+    later.extend(rest(T.jc0, lambda: (tj0, tj1), lambda: (t_cm, tg0)))
     tpk = vcp(T.pku[:], T.pk[:], i_k)
-    tuq = vq(T.uq[:], T.us[:], T.uin[:], du)
+    tuq = vqt(T.uq[:], T.us[:], T.uin[:], du)
+    fill(2)
+    unpacker(0)
     tu1 = vcp(T.uq2[:, 0:128].bitcast(dt.uint32), T.uq[:, 0:128].bitcast(dt.uint32).indirect(T.pku[:, 0:8]), tuq, tpk)
-    tu2 = vcp(T.us2[:, 0:128], T.us[:, 0:128].indirect(T.pku[:, 0:8]), tuq, tpk)
-    te = [vq(T.eq[:, 128 * b:128 * b + 128], T.es[:, 128 * b:128 * b + 128], T.ein[:, 3 - b:515 - b], i_e) for b in range(4)]
+    tu2 = acp(T.us2[:, 0:128], T.us[:, 0:128].indirect(T.pku[:, 0:8]), tuq, tpk)
+    fill(2)
+    unpacker(1)
+    fill(1)
+    unpacker(2)
+    unpacker(3)
+    fill()
+    send(0, R("lq", 0)[:, 0:C].bitcast(dt.uint8), T.xq0[:, 0:C].bitcast(dt.uint8), "arq0", *tx)
+    send(0, R("ls", 0)[:, 0:C], T.xs0[:, 0:C], "arq0", *tx)
 
-    def statics(r, tgm):
-        bg, mg, sm, lst = B("bg", r), B("mg", r), B("sm", r), B("lst", r)
-        t1 = vscan(bg[:, C:2 * C], T.keep[:], bg[:, 0:C], tgm, tkeep)
-        t2 = vcp(mg[:, 40:60], bg[:, C + 15:2 * C:16], t1)
-        t3 = vts(mg[:, 0:20], mg[:, 40:60], 9, Op.logical_shift_right, t2)
-        t4 = vts(mg[:, 20:40], mg[:, 40:60], 511, Op.bitwise_and, t2)
-        t5 = vtt(sm[:, 0:40], T.jc[:], mg[:, 0:40], Op.min, t4, t3, tjc)
-        t6 = vtt(sm[:, 40:80], T.jc[:], mg[:, 0:40], Op.max, t4, t3, tjc)
-        t7 = vcp(lst[:], sm[:, 0:80], t5, t6)
-        t8 = vtt(sm[:, 80:120], T.jc[:], mg[:, 0:40], Op.subtract, t4)
-        t9 = vts(sm[:, 120:160], sm[:, 80:120], 0.0, Op.is_lt, t8)
-        t10 = vtt(sm[:, 160:180], sm[:, 120:140], sm[:, 140:160], Op.is_equal, t9)
-        return t7, t10, t4
-
-    tgm = vtt(T.bg0[:, 0:C], T.gb0[:, 0:C].indirect(T.ciu[:, 0:20]), T.mask[:], Op.mult, tr2, tciu, tmask)
-    tl, tsm, tmg = statics(0, tgm)
-    twt = vts2(T.wts[:], T.t16[:], T.qf[:, 0:1], Op.not_equal, 4.0, Op.mult, i_t, tqf)
-    td = vts2(T.dia[:], T.t16[:, 0:16], T.qf[:, 0:1], Op.is_equal, 0.6, Op.mult, i_t, tqf)
-    tth = vscan(T.thr[:], T.fours[:], T.dia[:], fo, td)
-    tca = vcp(T.ca[:, 0:C].indirect(T.pu[:, 0:20]), T.crep[:], tcrep, tpu)
-    tcam = acp(T.cam[:], T.ca[:, 0:C].indirect(T.mu[:, 0:20]), tca, tmu)
-
-    def makeq(r, src, off, toff, *deps):
-        tb = B("tb", r)
-        t1 = vtt(tb[:, 0:C], src[:, 0:C].indirect(off), T.mask[:], Op.mult, toff, tmask, *deps)
-        t2 = vscan(tb[:, C:2 * C], T.keep[:], tb[:, 0:C], t1, tkeep)
-        return vts(B("qu", r)[:], tb[:, C + 15:2 * C:16], 160.0, Op.add, t2)
-
-    sent = [0]
-
-    def send(dst, out, src, sem, *deps):
-        need("G", deps)
-        rid, pid, _ = topo.addr(dst)
-        m = 0
-        for e in topo.engines(core, dst)[:8]:
-            m |= 1 << e
-        g.remote_dma(out, src, T.sem[sem], T.sem.sent, pid, rid, m)
-        sent[0] += 8
-
-    tq = None
-    t_tq = []
-    t_r = [()] * 4
-    tX = []
-    t_va = []
+    t_tq, t_rp, tX, tkp, tkk = [], [()] * 4, [], None, None
     for r in range(ROUNDS):
-        dst = T.cores[(rank + STEP[r]) % len(T.cores)]
-        xq, xs, lst, sm, mg = B("xq", r), B("xs", r), B("lst", r), B("sm", r), B("mg", r)
-        sc, ga, gb, bits, zz, li = B("sc", r), B("ga", r), B("gs", r), B("bits", r), B("zz", r), B("li", r)
-        send(dst, B("lq", r)[:, 0:C].bitcast(dt.uint8), xq[:, 0:C].bitcast(dt.uint8), "arr%d" % r, *tx)
-        send(dst, B("ls", r)[:, 0:C], xs[:, 0:C], "arr%d" % r, *tx)
-        ps = [mm(T.psb[:, 512 * h:512 * h + HX], T.uq2[:], T.us2[:], xq[:, HX * h:HX * h + HX], xs[:, HX * h:HX * h + HX], tx[h], tu1, tu2, *t_tq) for h in (0, 1)]
-        pt = [mm(T.psa[:, 512 * b:512 * b + C], T.eq[:, 128 * b:128 * b + 128], T.es[:, 128 * b:128 * b + 128], xq[:, 0:C], xs[:, 0:C], te[b], *tx, *t_r[b]) for b in range(4)]
-        ts0 = vcp(sc[:, 0:HX], T.psb[:, 0:HX], ps[0])
-        ts1 = acp(sc[:, HX:C], T.psb[:, 512:512 + HX], ps[1])
-        tga = acp(ga[:], sc[:, 0:C].indirect(lst[:, 20:40]), ts0, ts1, tl)
-        tgb = vcp(gb[:], sc[:, 0:C].indirect(lst[:, 0:20]), ts0, ts1, tl)
-        tb0 = vtt(bits[:, 0:C], sc[:, 0:C].indirect(lst[:, 40:60]), gb[:], Op.is_le, tgb)
-        tb1 = vtt(bits[:, C:2 * C], sc[:, 0:C].indirect(lst[:, 60:80]), ga[:], Op.is_le, tga)
-        tz = vscan(zz[:], T.wts[:], bits[:], twt, tb0, tb1)
-        e1 = vts(sm[:, 180:220], zz[:, 15:2 * C:16], T.thr[:, 15:16], Op.is_ge, tz, tth)
-        e2 = vtt(sm[:, 220:240], sm[:, 180:200], sm[:, 200:220], Op.is_equal, e1)
-        e3 = vtt(sm[:, 240:260], sm[:, 220:240], sm[:, 160:180], Op.is_equal, e2, tsm)
-        e4 = vtt(sm[:, 260:280], sm[:, 240:260], sm[:, 80:100], Op.mult, e3)
-        e5 = vtt(sm[:, 280:300], sm[:, 260:280], mg[:, 0:20], Op.add, e4)
-        phu = B("phu", r)
-        tphu = vcp(phu[:, 0:20], sm[:, 280:300], e5)
-        tt_ = [acp(T.tp[:, C * b:C * b + C], T.psa[:, 512 * b:512 * b + C], pt[b], *tX) for b in range(4)]
-        phr = B("phr", r)
-        tphr = acp(phr[:, 0:C], T.idb[:, 0:C].indirect(phu[:, 0:20]), tphu)
-        e6 = vtt(sm[:, 300:320], sm[:, 240:260], sm[:, 100:120], Op.mult, e3)
-        e7 = vtt(sm[:, 320:340], sm[:, 300:320], mg[:, 20:40], Op.add, e6)
-        tla = vcp(li[:, 0:20], sm[:, 320:340], e7)
-        if r == 0:
-            tq = makeq(0, T.cam, T.pu[:, 0:20], tpu, tcam)
-        tb = B("tb", r)
-        k1 = vtt(tb[:, 2 * C:3 * C], phr[:, 0:C].indirect(B("qu", r)[:, 0:20]), T.mask[:], Op.mult, tphr, tq)
-        k2 = vscan(tb[:, 3 * C:4 * C], T.keep[:], tb[:, 2 * C:3 * C], k1)
-        tlk = vts(li[:, 20:40], tb[:, 3 * C + 15:4 * C:16], 160.0, Op.add, k2)
-        send(dst, B("ll", r)[:], li[:], "arl%d" % r, tla, tlk)
-        if r + 1 < ROUNDS:
-            tcph = acp(phr[:, C:2 * C], T.crep[:, 0:C].indirect(phu[:, 0:20]), tphu, tcrep)
-            ta1 = acp(B("gb", r + 1)[:], T.w0[:, 0:C].indirect(li[:, 20:40]), tlk, tw0)
-            ta2 = acp(B("gb", r)[:] if r else T.kco[:], B("gb", r + 1)[:, 0:C].indirect(li[:, 0:20]), ta1, tla)
-            src = B("gb", r) if r else T.kco
-            tgm = vtt(B("bg", r + 1)[:, 0:C], src[:, 0:C].indirect(T.ciu[:, 0:20]), T.mask[:], Op.mult, ta2)
-            tl, tsm, tmg = statics(r + 1, tgm)
-            tm2 = vcp(B("phu", r + 1)[:, 20:40], B("mg", r + 1)[:, 0:20], tmg)
-        else:
-            ta1 = acp(B("gb", r)[:], T.idf[:, 0:C].indirect(li[:, 20:40]), tlk, i_f)
-            tco = acp(T.kco[:], B("gb", r)[:, 0:C].indirect(li[:, 0:20]), ta1, tla)
-            need("S", [tco])
-            g.sync.dma_start(T.co[:], T.kco[0:128:16, :]).then_inc(T.sem.ost, 16)
-        if r == 0:
-            tvq = vq(T.vq[:], T.vs[:], T.vin[:], dv)
-        arr, arl = ("arr%d" % r, 16), ("arl%d" % r, 8)
-        pq = [mm(T.psb[:, 512 * b:512 * b + C], T.eq[:, 128 * b:128 * b + 128], T.es[:, 128 * b:128 * b + 128], B("lq", r)[:], B("ls", r)[:], arr, ts0, ts1) for b in range(4)]
-        t_tq = [acp(T.tq[:, C * b:C * b + C], T.psb[:, 512 * b:512 * b + C], pq[b], *t_va, scale=0.5) for b in range(4)]
-        ll = B("ll", r)
-        tzr = t_z if r else []
-        t_cp, tv = {}, {}
-        for kind, b in ((("c", 0), ("c", 1), ("c", 2), ("c", 3), ("v", 0), ("v", 1), ("v", 2), ("v", 3)) if r == 0 else
-                        (("c", 0), ("c", 1), ("v", 0), ("c", 2), ("v", 1), ("c", 3), ("v", 2), ("v", 3))):
-            pl = slice(C * b, C * b + C)
-            if kind == "c":
-                t_cp[b] = vcp(T.tr[:, pl], T.tq[:, pl], t_tq[b])
-            else:
-                tv[b] = vtt(T.vp[:, pl], T.tq[:, pl].indirect(ll[:, 20:40]), T.tr[:, pl], Op.add, t_cp[b], arl, *tzr)
-        t_va = [tv[3]]
-        za = [acp(T.zt[:, b:4 * C:4], T.vp[:, C * b:C * b + C].indirect(ll[:, 0:20]), tv[b], arl) for b in range(3)]
-        z3 = vcp(T.zt[:, 3:4 * HZ:4], T.vp[:, 3 * C:4 * C].indirect(ll[:, 0:HZ // 16]), tv[3])
-        za.append(acp(T.zt[:, 4 * HZ + 3:4 * C:4], T.vp[:, 3 * C:4 * C].indirect(ll[:, HZ // 16:20]), tv[3]))
-        t_z = za + [z3]
-        zq, zs = B("zq", r), B("zs", r)
-        tz0 = vq(zq[:, 0:HZ], zs[:, 0:HZ], T.zt[:, 0:4 * HZ], z3, za[2])
-        tz1 = vq(zq[:, HZ:C], zs[:, HZ:C], T.zt[:, 4 * HZ:4 * C], z3, za[3])
         last = r + 1 == ROUNDS
-        order = [3, 0, 1, 2] if last else [0, 1, 2, 3]
-        pr = {}
-        for b in order:
-            pr[b] = mm(T.psa[:, 512 * b:512 * b + C], T.wq[:, 128 * b:128 * b + 128], T.wsc[:, 128 * b:128 * b + 128], zq[:], zs[:], dwc, dws, tz0, tz1, tt_[b])
-        if not last:
-            tcpm = acp(B("phr", r + 1)[:, C:2 * C] if False else B("cpm", r)[:], phr[:, C:2 * C].indirect(B("phu", r + 1)[:, 20:40]), tcph, tm2)
-        tr = {}
-        for b in order:
-            o, i = T.rp[:, C * b:C * b + C], T.psa[:, 512 * b:512 * b + C]
-            if last and b == 3:
-                tr[b] = vts(o, i, 0.03125, Op.mult, pr[b], *tX)
+        xq, xs, lst, sm, mg, vl, zl = R("xq", r), R("xs", r), T.lst, T.sm, T.mg, R("vl", r), R("zl", r)
+        lk, lv, lz = R("lk", r), R("lv", r), R("lz", r)
+        arq, ark, arv, arz = ("arq%d" % r, 16), ("ark%d" % r, 8), ("arv%d" % r, 8), ("arz%d" % r, 8)
+        ps = [mm(T.psb[:, 512 * h:512 * h + H], T.uq2[:], T.us2[:], xq[:, H * h:H * h + H], xs[:, H * h:H * h + H], tx[h], tu1, tu2, *t_tq) for h in (0, 1)]
+        pt = [mm(bank(T.psa, b), T.eq[:, w128(b)], T.es[:, w128(b)], xq[:, 0:C], xs[:, 0:C], *te, *tx, *t_rp[b]) for b in range(4)]
+        fill()
+        ts = [vcp(T.sc[:, 0:H], T.psb[:, 0:H], ps[0]), acp(T.sc[:, H:C], T.psb[:, 512:512 + H], ps[1])]
+        tl = st["l"]
+        tga = acp(T.ga[:], T.sc[:, 0:C].indirect(lst[:, 20:40]), *ts, tl)
+        tgb1 = acp(T.gb[:, H:C], T.sc[:, 0:C].indirect(lst[:, 10:20]), *ts, tl)
+        tgb0 = vcp(T.gb[:, 0:H], T.sc[:, 0:C].indirect(lst[:, 0:10]), *ts, tl)
+        ttp, kps = {}, {}
+        if r == 0:
+            def q0(): kps[1] = vtt(T.kg[:, 0:C], gat(T.am, T.pu), T.mask[:], Op.mult, tam, tmask)
+            def q1(): kps[2] = vscan(T.kg[:, C:2 * C], T.keep[:], T.kg[:, 0:C], kps[1], tkeep)
+            def q2(): kps[3] = vts(R("kp", 0)[:], T.kg[:, C + 15:2 * C:16], 2.0 ** -9, Op.mult, kps[2])
+            later.extend([q0, q1, q2])
+            fill(1)
+            for b in range(3):
+                ttp[b] = acp(T.tp[:, pl(b)], bank(T.psa, b), pt[b])
+        tb0 = vtt(T.bits[:, 0:H], T.sc[:, 0:C].indirect(lst[:, 40:50]), T.gb[:, 0:H], Op.is_le, tgb0)
+        tb2 = vtt(T.bits[:, C:2 * C], T.sc[:, 0:C].indirect(lst[:, 60:80]), T.ga[:], Op.is_le, tga)
+        tb1 = vtt(T.bits[:, H:C], T.sc[:, 0:C].indirect(lst[:, 50:60]), T.gb[:, H:C], Op.is_le, tgb1)
+        if r == 1:
+            kps, a, b, c = wrap16(T.ph[:, 3 * C:4 * C], T.ciu[:, 0:20], R("kp", 1)[:], 2 * C, tkk)
+            later.extend([a, b, c])
+        fill(1)
+        tz = vscan(T.zz[:], T.wts[:], T.bits[:], *twt, tb0, tb1, tb2)
+        fill(1)
+        e1 = vts(sm[:, 180:220], T.zz[:, 15:2 * C:16], T.thr[:, 15:16], Op.is_ge, tz, tth)
+        fill(1)
+        e2 = vtt(sm[:, 220:240], sm[:, 180:200], sm[:, 200:220], Op.is_equal, e1)
+        e3 = vtt(sm[:, 240:260], sm[:, 220:240], sm[:, 160:180], Op.is_equal, e2, st["q"])
+        e4 = vtt(sm[:, 260:280], sm[:, 240:260], sm[:, 80:100], Op.mult, e3, st["d"])
+        f4 = vtt(sm[:, 300:320], sm[:, 240:260], sm[:, 100:120], Op.mult, e3, st["d"])
+        e5 = vtt(sm[:, 280:300], sm[:, 260:280], mg[:, 0:20], Op.add, e4)
+        f5 = vtt(sm[:, 320:340], sm[:, 300:320], mg[:, 20:40], Op.add, f4)
+        tvl = vcp(vl[:], sm[:, 280:300], e5)
+        tap = vcp(T.ap[:] if r else T.thu[:], sm[:, 320:340], f5)
+        if r < 2:
+            tkp = kps[3]
+            send(r, R("lk", r)[:], R("kp", r)[:], "ark%d" % r, tkp)
+        send(r, R("lv", r)[:], vl[:], "arv%d" % r, tvl)
+
+        pq = [mm(bank(T.psb, b), T.eq[:, w128(b)], T.es[:, w128(b)], R("lq", r)[:], R("ls", r)[:], arq, *ts) for b in range(4)]
+        tq, tk, tv = {}, {}, {}
+
+        def pick(b): tk[b] = acp(T.tk[:, pl(b)], T.tq[:, pl(b)].indirect(lk[:, 0:20]), tq[b], ark)
+        def aevac(b): tq[b] = asc(T.tq[:, pl(b)], bank(T.psb, b), 0.5, pq[b])
+        def vevac(b): tq[b] = vts(T.tq[:, pl(b)], bank(T.psb, b), 0.5, Op.mult, pq[b])
+        def evac_own(b): ttp[b] = vcp(T.tp[:, pl(b)], bank(T.psa, b), pt[b])
+        def addv(b): tv[b] = vtt(T.vp[:, pl(b)], T.tq[:, pl(b)].indirect(lv[:, 0:20]), T.tk[:, pl(b)], Op.add, tq[b], tk[b], arv)
+        def zcols(b, c0, c1): return T.zt[:, 4 * c0 + b:4 * c1:4], T.vp[:, pl(b)].indirect(lz[:, c0 // 16:c1 // 16])
+
+        table = T.idf if last else T.w0
+
+        def next_lists():
+            def m(): st["m"] = vtt(T.bg[:, 0:C], gat(T.f1, T.ciu), T.mask[:], Op.mult, tf1, tci["u"])
+            def n0(): st[0] = vscan(T.bg[:, C:2 * C], T.keep[:], T.bg[:, 0:C], st["m"])
+            def n1(): st[1] = vcp(T.mg[:, 40:60], T.bg[:, C + 15:2 * C:16], st[0])
+            def n2(): st[2] = vts(T.mg[:, 0:20], T.mg[:, 40:60], 9, Op.logical_shift_right, st[1])
+            def n3(): st[3] = vts(T.mg[:, 20:40], T.mg[:, 40:60], 511, Op.bitwise_and, st[1])
+            def n4(): st[4] = vcp(T.m2u[:], T.mg[:, 0:20], st[2])
+            return [m, n0, n1, n2, n3, n4] + rest(T.jc, lambda: (tj, tci["f"]), lambda: (st[2], st[3]))
+
+        if r == 0:
+            tpp = vtt(T.pp[:], gat(T.am, T.pu), T.idf[:], Op.add, tam, i_f)
+            later.extend(inverse())
+            tt0 = acp(T.tpr[:], gat(T.pp, T.thu), tpp, tap)
+            for b in range(4):
+                aevac(b)
+                pick(b)
+            fill()
+            k1 = vtt(T.kg[:, 0:C], gat(T.tpr, T.ciu), T.mask[:], Op.mult, tt0, tci["u"])
+            tw0 = vtt(T.w0[:], gat(T.id512, T.cu), T.idf[:], Op.add, i_5, i_f, tcu)
+            k2 = vscan(T.kg[:, C:2 * C], T.keep[:], T.kg[:, 0:C], k1)
+            k3 = vcp(mg[:, 60:80], T.kg[:, C + 15:2 * C:16], k2)
+            k4 = vts(mg[:, 80:100], mg[:, 60:80], 9, Op.logical_shift_right, k3)
+            k5 = vts(mg[:, 100:120], mg[:, 60:80], 511, Op.bitwise_and, k3)
+            tzl = vcp(zl[:], mg[:, 80:100], k4)
+            tap = vcp(T.ap[:], mg[:, 100:120], k5)
+            send(0, R("lz", 0)[:], zl[:], "arz0", tzl)
+            tvq = vqt(T.vq[:], T.vs[:], T.vin[:], dv)
+            tf0 = acp(T.f0[:], gat(table, vl), tvl, tw0)
+            tf1 = acp(T.f1[:], gat(T.f0, zl), tf0, tzl)
+            for b in range(4):
+                addv(b)
+            later.extend(next_lists())
+        else:
+            fill()
+            if r == 1:
+                tpir = acp(T.pir[:], gat(T.crep, R("kp", 1)), tkp)
+            s, a, b, c = wrap16(T.pir[:, 0:C], vl[:, 0:20], zl[:], 0, tpir, tvl)
+            a()
+            evac_own(0)
+            b()
+            evac_own(1)
+            c()
+            tzl = s[3]
+            evac_own(2)
+            send(r, R("lz", r)[:], zl[:], "arz%d" % r, tzl)
+            tf0 = acp(T.f0[:], gat(table, vl), tvl, tw0, i_f)
+            if last:
+                tco = acp(T.kco[:], gat(T.f0, zl), tf0, tzl)
+                need("S", [tco])
+                g.sync.dma_start(T.co[:], T.kco[0:128:16, :]).then_inc(T.sem.ost, 16)
             else:
-                tr[b] = acp(o, i, pr[b], *tX, scale=0.03125)
-        t_r = [[tr[b]] for b in range(4)]
+                tph = acp(T.ph[:, 0:C], gat(T.idb, vl), tvl, i_b)
+                tf1 = acp(T.f1[:], gat(T.f0, zl), tf0, tzl)
+                later.extend(next_lists())
+                fill(3)
+            aevac(0)
+            pick(0)
+            vevac(1)
+            fill(3)
+            vevac(2)
+            fill(1)
+            vevac(3)
+            fill(1)
+            pick(1)
+            pick(2)
+            pick(3)
+            if not last:
+                tkk = acp(T.ph[:, C:2 * C], T.ph[:, 0:C].indirect(T.m2u[:, 0:20]), tph, st[4])
+            for b in range(4):
+                addv(b)
+                fill(1)
+        t_tq = [tq[b] for b in range(4)]
+        za = [acp(*zcols(0, 0, C), tv[0], arz), acp(*zcols(1, 0, C), tv[1]), acp(*zcols(2, 0, HZ), tv[2])]
+        zv = [vcp(*zcols(2, HZ, C), tv[2], arz), vcp(*zcols(3, HZ, C), tv[3]), vcp(*zcols(3, 0, HZ), tv[3])]
+        tz1 = vqt(T.zq[:, HZ:C], T.zs[:, HZ:C], T.zt[:, 4 * HZ:4 * C], *zv, za[1])
+        tz0 = vqt(T.zq[:, 0:HZ], T.zs[:, 0:HZ], T.zt[:, 0:4 * HZ], *zv, *za)
+        order = [0, 1, 3, 2]
+        pr, tr = {}, {}
+        for b in order:
+            pr[b] = mm(bank(T.psb if b == 3 else T.psa, b), T.wq[:, w128(b)], T.wsc[:, w128(b)], T.zq[:], T.zs[:], dwc, dws, tz0, tz1, tq[3] if b == 3 else ttp[b])
+        if r == 0:
+            tph = acp(T.ph[:, 0:C], gat(T.idb, vl), tvl, i_b)
+            tkk = acp(T.ph[:, C:2 * C], T.ph[:, 0:C].indirect(vl[:, 0:20]), tph)
+            fill(2)
+        elif not last:
+            tkk = acp(T.ph[:, 3 * C:4 * C], T.ph[:, C:2 * C].indirect(vl[:, 0:20]), tkk)
+            kp = R("kp", r + 1)
+            s, a, b, c = wrap16(T.ph[:, 3 * C:4 * C], T.ciu[:, 0:20], kp[:], 2 * C, tkk)
+            a()
+            fill(1)
+            b()
+            fill(1)
+            c()
+            tkp = s[3]
+            send(r + 1, R("lk", r + 1)[:], kp[:], "ark%d" % (r + 1), tkp)
+        for b in order:
+            tr[b] = asc(T.rp[:, pl(b)], bank(T.psb if b == 3 else T.psa, b), 0.03125, pr[b], *tX)
+        trg = acp(T.rg[:], T.rp[:, pl(3)].indirect(T.ap[:, 0:20]), tr[3], tap)
+        if r == 0:
+            tkk = acp(T.ph[:, 2 * C:3 * C], T.ph[:, C:2 * C].indirect(zl[:, 0:20]), tkk, tzl)
+            tkk = acp(T.ph[:, 3 * C:4 * C], T.ph[:, 2 * C:3 * C].indirect(T.ap[:, 0:20]), tkk, tap)
+        elif not last:
+            tpir = acp(T.pir[:], gat(T.crep, kp), tkp)
+        tX = []
+        for b in range(3):
+            tX.append(vtt(T.xt[:, b:4 * C:4], T.rp[:, pl(b)].indirect(T.ap[:, 0:20]), T.tp[:, pl(b)], Op.add, tr[b], ttp[b], tap))
+            fill(2 if r == 0 else 1)
+        tX.append(vtt(T.xt[:, 3:4 * C:4], T.rg[:], bank(T.psa, 3), Op.add, trg, pt[3]))
+        t_rp = [[tr[0]], [tr[1]], [tr[2]], [tX[3]]]
+        t_tq = t_tq + [tr[3]]
+        nq, ns = R("xq", r + 1), R("xs", r + 1)
+        fill(1)
+        tx = [vqt(nq[:, h:h + H], ns[:, h:h + H], T.xt[:, 4 * h:4 * (h + H)], *tX) for h in (0, H)]
         if not last:
-            tq = makeq(r + 1, B("cpm", r), phu[:, 0:20], tphu, tcpm)
-        tX = [vtt(T.xt[:, b:4 * C:4], T.rp[:, C * b:C * b + C].indirect(li[:, 0:20]), T.tp[:, C * b:C * b + C], Op.add, tr[b], tt_[b], tla) for b in order]
-        nq, ns = B("xq", r + 1), B("xs", r + 1)
-        tx = [vq(nq[:, h:h + HX], ns[:, h:h + HX], T.xt[:, 4 * h:4 * (h + HX)], *tX) for h in (0, HX)]
+            n = r + 1
+            send(n, R("lq", n)[:, 0:C].bitcast(dt.uint8), nq[:, 0:C].bitcast(dt.uint8), "arq%d" % n, *tx)
+            send(n, R("ls", n)[:, 0:C], ns[:, 0:C], "arq%d" % n, *tx)
 
     need("S", tx)
     g.sync.dma_start(T.oc[:, 0:4 * C], T.xq3[:, 0:C].bitcast(dt.uint8)).then_inc(T.sem.ost, 16)
     for k in range(4):
         g.sync.dma_start(T.osc[4 * k:4 * k + 4, 0:C], T.xs3[32 * k:32 * k + 4, 0:C]).then_inc(T.sem.ost, 16)
-    py = [mm(T.psb[:, 512 * h:512 * h + HX], T.vq[:], T.vs[:], T.xq3[:, HX * h:HX * h + HX], T.xs3[:, HX * h:HX * h + HX], tx[h], tvq, *t_tq) for h in (0, 1)]
-    ty0 = vcp(T.yt[:, 0:HX], T.psb[:, 0:HX], py[0])
-    ty1 = acp(T.yt[:, HX:C], T.psb[:, 512:512 + HX], py[1])
+    py = [mm(T.psb[:, 512 * h:512 * h + H], T.vq[:], T.vs[:], T.xq3[:, H * h:H * h + H], T.xs3[:, H * h:H * h + H], tx[h], tvq, *t_tq) for h in (0, 1)]
+    ty0 = vcp(T.yt[:, 0:H], T.psb[:, 0:H], py[0])
+    ty1 = acp(T.yt[:, H:C], T.psb[:, 512:512 + H], py[1])
     need("A", [ty0, ty1])
     g.scalar.dma_start(T.y[:], T.yt[:]).then_inc(T.sem.ost, 16)
     need("G", [(q, count[q]) for q in ("V", "A", "P", "G")])
     g.wait_ge(T.sem.ost, 16 * 7)
     g.wait_ge(T.sem.sent, sent[0])
-
-
-for _r in range(ROUNDS):
-    SCRATCH["gs%d" % _r] = ("sbuf", [128, C], "float32")
-    SCRATCH["phr%d" % _r] = ("sbuf", [128, 2 * C], "bfloat16")
-    SCRATCH["phu%d" % _r] = ("sbuf", [128, 40], "uint16")
-    if _r < ROUNDS - 1:
-        SCRATCH["cpm%d" % _r] = ("sbuf", [128, C], "bfloat16")

@@ -6,18 +6,19 @@ H = C // 2
 STEP = [1, 2, 4]
 ROUNDS = 3
 HZ = 192
+S0 = 2.0 ** -70
 X4, F32, B16, I32, U16, U8 = "float8_e4m3fn_x4", "float32", "bfloat16", "int32", "uint16", "uint8"
 
 SCRATCH = {}
 for _names, _w, _d in (
-        ("idf id512", C, F32), ("idb mask keep t16", C, B16), ("wts", 2 * C, B16), ("pcol qi", 1, I32), ("qf", 1, F32),
-        ("c16", 20, F32), ("pk", 8, I32), ("pku", 8, U16), ("fours dia", 16, B16), ("thr", 16, F32), ("ein", 516, B16),
+        ("idf id512 ids", C, F32), ("idb mask keep t16 w1k", C, B16), ("wts", 2 * C, B16), ("pcol qi", 1, I32), ("qf", 1, F32),
+        ("c16", 20, F32), ("pk", 8, I32), ("pku", 8, U16), ("fours dia less dib", 16, B16), ("thr inv", 16, F32), ("ein", 516, B16),
         ("eq", 512, X4), ("es", 512, U8),
         ("xin", 4 * C, B16), ("uin vin", 512, B16), ("ci32 mi32 pi32", 20, I32), ("cu mu pu", 20, U16),
         ("wq", 512, X4), ("wsc", 512, U8), ("uq uq2 vq", 128, X4), ("us us2 vs", 128, U8),
-        ("cir cim ciz crep", C, B16), ("ciu ap thu m2u", 20, U16), ("jc jc0", 40, F32), ("w0 an am pp pir tpr", C, F32),
-        ("sc ga gb f0 f1 kco yt rg", C, F32), ("bits zz", 2 * C, B16), ("lst", 80, U16), ("sm", 340, F32), ("mg", 120, I32),
-        ("bg kg", 2 * C, F32), ("ph", 4 * C, B16), ("tb", 4 * C, B16),
+        ("crep thb an am pp tpr", C, B16), ("cir w0 pir", C, F32), ("wx", 14 * C, F32), ("ciu ap thu m2u", 20, U16), ("jc jc0", 40, F32),
+        ("sc ga gb f0 f1 kco yt rg", C, F32), ("bits zz", 2 * C, B16), ("lst", 80, U16), ("sm", 340, F32), ("mg", 60, I32),
+        ("bg", 2 * C, F32), ("ph", 4 * C, B16), ("tb", 4 * C, B16),
         ("tp vp rp", 4 * C, F32), ("tq tk zt xt", 4 * C, B16), ("zq", C, X4), ("zs", C, U8)):
     for _n in _names.split():
         SCRATCH[_n] = ("sbuf", [128, _w], _d)
@@ -100,8 +101,8 @@ def rank_program(g, core, T, topo):
             later.pop(0)()
 
     dc = load(g.scalar, "cl", T.ci32[:], T.cl[:])
-    dm = load(g.scalar, "ml", T.mi32[:], T.ml[:])
     dp = load(g.scalar, "pl", T.pi32[:], T.pl[:])
+    dm = load(g.scalar, "ml", T.mi32[:], T.ml[:])
     dx = load(g.sync, "x", T.xin[:], T.x[:])
     du = load(g.sync, "u", T.uin[:], T.u[:])
     dwc = load(g.sync, "wc", T.wq[:].bitcast(dt.uint8), T.wc[:])
@@ -115,12 +116,12 @@ def rank_program(g, core, T, topo):
     i_c = iota(T.c16, [[16, 20]], 0, 0)
     i_t = iota(T.t16, [[0, 20], [1, 16]], 0, 0)
     i_b = iota(T.idb, [[1, C]], -160, 0)
-    i_5 = iota(T.id512, [[512, C]], 0, 0)
     i_k = iota(T.pk, [[16, 8]], 0, 0, False)
     t_e1 = vfill(T.ein[:], 1.0)
     t_fo = vfill(T.fours[:], 4.0)
     i_e = run("G", [t_e1], g.affine_select, T.ein[:], T.ein[:], [[1, 516]], Op.is_equal, 0.0, -3, -4)
     i_f = iota(T.idf, [[1, C]], 0, 0)
+    i_5 = iota(T.id512, [[512, C]], 0, 0)
 
     tqi = vts(T.qi[:], T.pcol[:], 15, Op.bitwise_and, i_p)
     tqf = vcp(T.qf[:], T.qi[:], tqi)
@@ -131,11 +132,17 @@ def rank_program(g, core, T, topo):
     twt = [vts2(T.wts[:, h:h + C], T.t16[:], T.qf[:, 0:1], Op.not_equal, 4.0, Op.mult, i_t, tqf) for h in (0, C)]
     tdi = vts2(T.dia[:], T.t16[:, 0:16], T.qf[:, 0:1], Op.is_equal, 0.6, Op.mult, i_t, tqf)
     tth = vscan(T.thr[:], T.fours[:], T.dia[:], t_fo, tdi)
+    tw1 = vts2(T.w1k[:], T.t16[:], T.qf[:, 0:1], Op.is_gt, 1024.0, Op.mult, i_t, tqf)
+    tdj = vts2(T.dib[:], T.t16[:, 0:16], T.qf[:, 0:1], Op.is_equal, 1.0 / S0, Op.mult, i_t, tqf)
+    t_le = vfill(T.less[:], 2.0 ** -10)
+    tinv = vscan(T.inv[:], T.less[:], T.dib[:], t_le, tdj)
     tcu = vcp(T.cu[:], T.ci32[:], dc)
     tj1 = vcp(T.jc0[:, 0:20], T.ci32[:], dc)
+    tcrep = acp(T.crep[:], gat(T.idb, T.cu), i_b, tcu)
+    tpu = vcp(T.pu[:], T.pi32[:], dp)
+    tan = vcp(T.an[:, 0:C].indirect(T.pu[:, 0:20]), T.idb[:], i_b, tpu)
     tmu = vcp(T.mu[:], T.mi32[:], dm)
     tg0 = vcp(T.mg[:, 20:40], T.mi32[:], dm)
-    tcrep = acp(T.crep[:], gat(T.idb, T.cu), i_b, tcu)
 
     def wrap16(src, off, out, col, *deps):
         s = {}
@@ -143,6 +150,15 @@ def rank_program(g, core, T, topo):
         def b(): s[2] = vscan(T.tb[:, col + C:col + 2 * C], T.keep[:], T.tb[:, col:col + C], s[1], tkeep)
         def c(): s[3] = vts(out, T.tb[:, col + C + 15:col + 2 * C:16], 160.0, Op.add, s[2])
         return s, a, b, c
+
+    def pickx(i, src, off, *deps):
+        return run("A", deps, g.scalar.activation, T.wx[:, 2 * C * i:2 * C * i + C], src.indirect(off), Fn.Identity, bias=160 * S0, scale=S0)
+
+    def scanx(i, src, *deps):
+        return vscan(T.wx[:, 2 * C * i + C:2 * C * i + 2 * C], T.w1k[:], src if src is not None else T.wx[:, 2 * C * i:2 * C * i + C], tw1, *deps)
+
+    def readx(i, out, tok):
+        return vts2(out, T.wx[:, 2 * C * i + C + 15:2 * C * i + 2 * C:16], T.inv[:, 15:16], Op.mult, 0.05, Op.add, tok, tinv)
 
     st = {}
 
@@ -163,35 +179,24 @@ def rank_program(g, core, T, topo):
 
     def inverse():
         s = {}
-        def o(): s[0] = vcp(T.cir[:, 0:C].indirect(T.cu[:, 0:20]), T.idb[:], i_b, tcu)
-        def a(): s[1] = vtt(T.cim[:], T.cir[:], T.mask[:], Op.mult, s[0], tmask)
-        def b(): s[2] = vscan(T.ciz[:], T.keep[:], T.cim[:], s[1], tkeep)
-        def c(): tci["u"] = vts(T.ciu[:], T.ciz[:, 15:C:16], 160.0, Op.add, s[2])
-        def d(): tci["f"] = vts(T.jc[:, 20:40], T.ciz[:, 15:C:16], 160.0, Op.add, s[2])
-        return [o, a, b, c, d]
+        def o(): s[0] = vcp(T.cir[:, 0:C].indirect(T.cu[:, 0:20]), T.ids[:], tids, tcu)
+        def b(): s[2] = scanx(2, T.cir[:], s[0])
+        def c(): tci["u"] = readx(2, T.ciu[:], s[2])
+        return [o, b, c]
 
-    tpu = vcp(T.pu[:], T.pi32[:], dp)
-    s, a, b, c = wrap16(T.crep[:, 0:C], T.mu[:, 0:20], T.mg[:, 0:20], 0, tcrep, tmu)
-    a()
-    tan = vcp(T.an[:, 0:C].indirect(T.pu[:, 0:20]), T.id512[:], i_5, tpu)
+    tx_cm = pickx(0, T.crep[:, 0:C], T.mu[:, 0:20], tcrep, tmu)
     tam = acp(T.am[:], gat(T.an, T.mu), tan, tmu)
-    b()
-    tx = [vqt(T.xq0[:, 0:H], T.xs0[:, 0:H], T.xin[:, 0:2 * C], dx)]
-    c()
-    tx.append(vqt(T.xq0[:, H:C], T.xs0[:, H:C], T.xin[:, 2 * C:4 * C], dx))
-    t_cm = s[3]
-    later.extend(rest(T.jc0, lambda: (tj0, tj1), lambda: (t_cm, tg0)))
+    tx_kp = pickx(1, T.am[:, 0:C], T.pu[:, 0:20], tam)
+    tx = [vqt(T.xq0[:, h:h + H], T.xs0[:, h:h + H], T.xin[:, 4 * h:4 * (h + H)], dx) for h in (0, H)]
+    t_cm = scanx(0, None, tx_cm)
     tpk = vcp(T.pku[:], T.pk[:], i_k)
     tuq = vqt(T.uq[:], T.us[:], T.uin[:], du)
+    t_cm = readx(0, T.mg[:, 0:20], t_cm)
+    later.extend(rest(T.jc0, lambda: (tj0, tj1), lambda: (t_cm, tg0)))
     fill(2)
-    unpacker(0)
     tu1 = vcp(T.uq2[:, 0:128].bitcast(dt.uint32), T.uq[:, 0:128].bitcast(dt.uint32).indirect(T.pku[:, 0:8]), tuq, tpk)
     tu2 = acp(T.us2[:, 0:128], T.us[:, 0:128].indirect(T.pku[:, 0:8]), tuq, tpk)
-    fill(2)
-    unpacker(1)
-    fill(1)
-    unpacker(2)
-    unpacker(3)
+    tids = asc(T.ids[:], T.idf[:], S0, i_f)
     fill()
     send(0, R("lq", 0)[:, 0:C].bitcast(dt.uint8), T.xq0[:, 0:C].bitcast(dt.uint8), "arq0", *tx)
     send(0, R("ls", 0)[:, 0:C], T.xs0[:, 0:C], "arq0", *tx)
@@ -202,54 +207,62 @@ def rank_program(g, core, T, topo):
         xq, xs, lst, sm, mg, vl, zl = R("xq", r), R("xs", r), T.lst, T.sm, T.mg, R("vl", r), R("zl", r)
         lk, lv, lz = R("lk", r), R("lv", r), R("lz", r)
         arq, ark, arv, arz = ("arq%d" % r, 16), ("ark%d" % r, 8), ("arv%d" % r, 8), ("arz%d" % r, 8)
+
+        def own(b): return mm(bank(T.psa, b), T.eq[:, w128(b)], T.es[:, w128(b)], xq[:, 0:C], xs[:, 0:C], te[b], *tx, *t_rp[b])
+
         ps = [mm(T.psb[:, 512 * h:512 * h + H], T.uq2[:], T.us2[:], xq[:, H * h:H * h + H], xs[:, H * h:H * h + H], tx[h], tu1, tu2, *t_tq) for h in (0, 1)]
-        pt = [mm(bank(T.psa, b), T.eq[:, w128(b)], T.es[:, w128(b)], xq[:, 0:C], xs[:, 0:C], *te, *tx, *t_rp[b]) for b in range(4)]
+        if r:
+            pt = [own(b) for b in range(4)]
         fill()
         ts = [vcp(T.sc[:, 0:H], T.psb[:, 0:H], ps[0]), acp(T.sc[:, H:C], T.psb[:, 512:512 + H], ps[1])]
+        if r:
+            tkp = scanx(4 + r, None, tx_kp)
         tl = st["l"]
         tga = acp(T.ga[:], T.sc[:, 0:C].indirect(lst[:, 20:40]), *ts, tl)
         tgb1 = acp(T.gb[:, H:C], T.sc[:, 0:C].indirect(lst[:, 10:20]), *ts, tl)
         tgb0 = vcp(T.gb[:, 0:H], T.sc[:, 0:C].indirect(lst[:, 0:10]), *ts, tl)
         ttp, kps = {}, {}
-        if r == 0:
-            def q0(): kps[1] = vtt(T.kg[:, 0:C], gat(T.am, T.pu), T.mask[:], Op.mult, tam, tmask)
-            def q1(): kps[2] = vscan(T.kg[:, C:2 * C], T.keep[:], T.kg[:, 0:C], kps[1], tkeep)
-            def q2(): kps[3] = vts(R("kp", 0)[:], T.kg[:, C + 15:2 * C:16], 2.0 ** -9, Op.mult, kps[2])
-            later.extend([q0, q1, q2])
-            fill(1)
+        if r:
+            tkp = readx(4 + r, R("kp", r)[:], tkp)
+            send(r, R("lk", r)[:], R("kp", r)[:], "ark%d" % r, tkp)
+            tpir = acp(T.pir[:], gat(T.crep, R("kp", r)), tkp)
             for b in range(3):
-                ttp[b] = acp(T.tp[:, pl(b)], bank(T.psa, b), pt[b])
+                ttp[b] = acp(T.tp[:, pl(b)], bank(T.psa, b), pt[b], *tX)
+        else:
+            tpp = acp(T.pp[:], gat(T.am, T.pu), tam)
+            def q1(): kps[2] = scanx(1, None, tx_kp)
+            def q2(): kps[3] = readx(1, R("kp", 0)[:], kps[2])
+            later.extend([q1, lambda: unpacker(0), q2] + [lambda b=b: unpacker(b) for b in range(1, 4)])
+            fill(1)
         tb0 = vtt(T.bits[:, 0:H], T.sc[:, 0:C].indirect(lst[:, 40:50]), T.gb[:, 0:H], Op.is_le, tgb0)
         tb2 = vtt(T.bits[:, C:2 * C], T.sc[:, 0:C].indirect(lst[:, 60:80]), T.ga[:], Op.is_le, tga)
         tb1 = vtt(T.bits[:, H:C], T.sc[:, 0:C].indirect(lst[:, 50:60]), T.gb[:, H:C], Op.is_le, tgb1)
-        if r == 1:
-            kps, a, b, c = wrap16(T.ph[:, 3 * C:4 * C], T.ciu[:, 0:20], R("kp", 1)[:], 2 * C, tkk)
-            later.extend([a, b, c])
         fill(1)
         tz = vscan(T.zz[:], T.wts[:], T.bits[:], *twt, tb0, tb1, tb2)
         fill(1)
         e1 = vts(sm[:, 180:220], T.zz[:, 15:2 * C:16], T.thr[:, 15:16], Op.is_ge, tz, tth)
         fill(1)
         e2 = vtt(sm[:, 220:240], sm[:, 180:200], sm[:, 200:220], Op.is_equal, e1)
+        fill(1)
         e3 = vtt(sm[:, 240:260], sm[:, 220:240], sm[:, 160:180], Op.is_equal, e2, st["q"])
+        fill(1)
         e4 = vtt(sm[:, 260:280], sm[:, 240:260], sm[:, 80:100], Op.mult, e3, st["d"])
         f4 = vtt(sm[:, 300:320], sm[:, 240:260], sm[:, 100:120], Op.mult, e3, st["d"])
+        fill(1)
         e5 = vtt(sm[:, 280:300], sm[:, 260:280], mg[:, 0:20], Op.add, e4)
         f5 = vtt(sm[:, 320:340], sm[:, 300:320], mg[:, 20:40], Op.add, f4)
         tvl = vcp(vl[:], sm[:, 280:300], e5)
         tap = vcp(T.ap[:] if r else T.thu[:], sm[:, 320:340], f5)
-        if r < 2:
-            tkp = kps[3]
-            send(r, R("lk", r)[:], R("kp", r)[:], "ark%d" % r, tkp)
+        if r == 0:
+            send(0, R("lk", 0)[:], R("kp", 0)[:], "ark0", kps[3])
         send(r, R("lv", r)[:], vl[:], "arv%d" % r, tvl)
 
-        pq = [mm(bank(T.psb, b), T.eq[:, w128(b)], T.es[:, w128(b)], R("lq", r)[:], R("ls", r)[:], arq, *ts) for b in range(4)]
+        def neighbour(): return [mm(bank(T.psb, b), T.eq[:, w128(b)], T.es[:, w128(b)], R("lq", r)[:], R("ls", r)[:], arq, *ts) for b in range(4)]
         tq, tk, tv = {}, {}, {}
 
         def pick(b): tk[b] = acp(T.tk[:, pl(b)], T.tq[:, pl(b)].indirect(lk[:, 0:20]), tq[b], ark)
         def aevac(b): tq[b] = asc(T.tq[:, pl(b)], bank(T.psb, b), 0.5, pq[b])
         def vevac(b): tq[b] = vts(T.tq[:, pl(b)], bank(T.psb, b), 0.5, Op.mult, pq[b])
-        def evac_own(b): ttp[b] = vcp(T.tp[:, pl(b)], bank(T.psa, b), pt[b])
         def addv(b): tv[b] = vtt(T.vp[:, pl(b)], T.tq[:, pl(b)].indirect(lv[:, 0:20]), T.tk[:, pl(b)], Op.add, tq[b], tk[b], arv)
         def zcols(b, c0, c1): return T.zt[:, 4 * c0 + b:4 * c1:4], T.vp[:, pl(b)].indirect(lz[:, c0 // 16:c1 // 16])
 
@@ -262,111 +275,100 @@ def rank_program(g, core, T, topo):
             def n2(): st[2] = vts(T.mg[:, 0:20], T.mg[:, 40:60], 9, Op.logical_shift_right, st[1])
             def n3(): st[3] = vts(T.mg[:, 20:40], T.mg[:, 40:60], 511, Op.bitwise_and, st[1])
             def n4(): st[4] = vcp(T.m2u[:], T.mg[:, 0:20], st[2])
-            return [m, n0, n1, n2, n3, n4] + rest(T.jc, lambda: (tj, tci["f"]), lambda: (st[2], st[3]))
+            return [m, n0, n1, n2] + ([n4] if r else []) + [n3] + rest(T.jc, lambda: (tj, tci["f"]), lambda: (st[2], st[3]))
 
         if r == 0:
-            tpp = vtt(T.pp[:], gat(T.am, T.pu), T.idf[:], Op.add, tam, i_f)
             later.extend(inverse())
+            pt = [own(b) for b in range(4)]
+            for b in range(3):
+                ttp[b] = acp(T.tp[:, pl(b)], bank(T.psa, b), pt[b])
             tt0 = acp(T.tpr[:], gat(T.pp, T.thu), tpp, tap)
-            for b in range(4):
-                aevac(b)
-                pick(b)
+            tthb = acp(T.thb[:], gat(T.idb, T.thu), tap)
+            pq = neighbour()
+            tph = acp(T.ph[:, 0:C], gat(T.idb, vl), tvl, i_b)
+            tkk = acp(T.ph[:, C:2 * C], T.ph[:, 0:C].indirect(vl[:, 0:20]), tph)
+            aevac(0)
+            aevac(1)
+            pick(0)
             fill()
-            k1 = vtt(T.kg[:, 0:C], gat(T.tpr, T.ciu), T.mask[:], Op.mult, tt0, tci["u"])
-            tw0 = vtt(T.w0[:], gat(T.id512, T.cu), T.idf[:], Op.add, i_5, i_f, tcu)
-            k2 = vscan(T.kg[:, C:2 * C], T.keep[:], T.kg[:, 0:C], k1)
-            k3 = vcp(mg[:, 60:80], T.kg[:, C + 15:2 * C:16], k2)
-            k4 = vts(mg[:, 80:100], mg[:, 60:80], 9, Op.logical_shift_right, k3)
-            k5 = vts(mg[:, 100:120], mg[:, 60:80], 511, Op.bitwise_and, k3)
-            tzl = vcp(zl[:], mg[:, 80:100], k4)
-            tap = vcp(T.ap[:], mg[:, 100:120], k5)
-            send(0, R("lz", 0)[:], zl[:], "arz0", tzl)
-            tvq = vqt(T.vq[:], T.vs[:], T.vin[:], dv)
-            tf0 = acp(T.f0[:], gat(table, vl), tvl, tw0)
-            tf1 = acp(T.f1[:], gat(T.f0, zl), tf0, tzl)
-            for b in range(4):
-                addv(b)
-            later.extend(next_lists())
-        else:
-            fill()
-            if r == 1:
-                tpir = acp(T.pir[:], gat(T.crep, R("kp", 1)), tkp)
-            s, a, b, c = wrap16(T.pir[:, 0:C], vl[:, 0:20], zl[:], 0, tpir, tvl)
+            pick(1)
+            s, a, b, c = wrap16(T.tpr[:, 0:C], T.ciu[:, 0:20], zl[:], 0, tt0, tci["u"])
+            s2, a2, b2, c2 = wrap16(T.thb[:, 0:C], T.ciu[:, 0:20], T.ap[:], 2 * C, tthb, tci["u"])
             a()
-            evac_own(0)
+            tci["f"] = vcp(T.jc[:, 20:40], T.ciu[:], tci["u"])
             b()
-            evac_own(1)
             c()
             tzl = s[3]
-            evac_own(2)
+            send(0, R("lz", 0)[:], zl[:], "arz0", tzl)
+            a2()
+            tw0 = vtt(T.w0[:], gat(T.id512, T.cu), T.idf[:], Op.add, i_5, i_f, tcu)
+            b2()
+            vevac(2)
+            c2()
+            vevac(3)
+            tap = s2[3]
+            pick(2)
+            pick(3)
+            tf0 = acp(T.f0[:], gat(table, vl), tvl, tw0)
+        else:
+            pq = neighbour()
+            fill()
+            s, a, b, c = wrap16(T.pir[:, 0:C], vl[:, 0:20], zl[:], 0, tpir, tvl)
+            a()
+            b()
+            c()
+            tzl = s[3]
             send(r, R("lz", r)[:], zl[:], "arz%d" % r, tzl)
             tf0 = acp(T.f0[:], gat(table, vl), tvl, tw0, i_f)
             if last:
-                tco = acp(T.kco[:], gat(T.f0, zl), tf0, tzl)
-                need("S", [tco])
-                g.sync.dma_start(T.co[:], T.kco[0:128:16, :]).then_inc(T.sem.ost, 16)
+                tvq = vqt(T.vq[:], T.vs[:], T.vin[:], dv)
             else:
                 tph = acp(T.ph[:, 0:C], gat(T.idb, vl), tvl, i_b)
-                tf1 = acp(T.f1[:], gat(T.f0, zl), tf0, tzl)
-                later.extend(next_lists())
-                fill(3)
             aevac(0)
-            pick(0)
             vevac(1)
-            fill(3)
+            pick(0)
             vevac(2)
-            fill(1)
-            vevac(3)
-            fill(1)
             pick(1)
+            vevac(3)
             pick(2)
             pick(3)
-            if not last:
-                tkk = acp(T.ph[:, C:2 * C], T.ph[:, 0:C].indirect(T.m2u[:, 0:20]), tph, st[4])
-            for b in range(4):
-                addv(b)
-                fill(1)
+        for b in range(4):
+            addv(b)
         t_tq = [tq[b] for b in range(4)]
         za = [acp(*zcols(0, 0, C), tv[0], arz), acp(*zcols(1, 0, C), tv[1]), acp(*zcols(2, 0, HZ), tv[2])]
         zv = [vcp(*zcols(2, HZ, C), tv[2], arz), vcp(*zcols(3, HZ, C), tv[3]), vcp(*zcols(3, 0, HZ), tv[3])]
         tz1 = vqt(T.zq[:, HZ:C], T.zs[:, HZ:C], T.zt[:, 4 * HZ:4 * C], *zv, za[1])
         tz0 = vqt(T.zq[:, 0:HZ], T.zs[:, 0:HZ], T.zt[:, 0:4 * HZ], *zv, *za)
+        if last:
+            tco = acp(T.kco[:], gat(T.f0, zl), tf0, tzl)
+            need("S", [tco])
+            g.sync.dma_start(T.co[:], T.kco[0:128:16, :]).then_inc(T.sem.ost, 16)
+        else:
+            tf1 = acp(T.f1[:], gat(T.f0, zl), tf0, tzl)
+            later.extend(next_lists())
         order = [0, 1, 3, 2]
         pr, tr = {}, {}
         for b in order:
             pr[b] = mm(bank(T.psb if b == 3 else T.psa, b), T.wq[:, w128(b)], T.wsc[:, w128(b)], T.zq[:], T.zs[:], dwc, dws, tz0, tz1, tq[3] if b == 3 else ttp[b])
-        if r == 0:
-            tph = acp(T.ph[:, 0:C], gat(T.idb, vl), tvl, i_b)
-            tkk = acp(T.ph[:, C:2 * C], T.ph[:, 0:C].indirect(vl[:, 0:20]), tph)
-            fill(2)
-        elif not last:
-            tkk = acp(T.ph[:, 3 * C:4 * C], T.ph[:, C:2 * C].indirect(vl[:, 0:20]), tkk)
-            kp = R("kp", r + 1)
-            s, a, b, c = wrap16(T.ph[:, 3 * C:4 * C], T.ciu[:, 0:20], kp[:], 2 * C, tkk)
-            a()
-            fill(1)
-            b()
-            fill(1)
-            c()
-            tkp = s[3]
-            send(r + 1, R("lk", r + 1)[:], kp[:], "ark%d" % (r + 1), tkp)
+        fill(2)
         for b in order:
             tr[b] = asc(T.rp[:, pl(b)], bank(T.psb if b == 3 else T.psa, b), 0.03125, pr[b], *tX)
         trg = acp(T.rg[:], T.rp[:, pl(3)].indirect(T.ap[:, 0:20]), tr[3], tap)
-        if r == 0:
-            tkk = acp(T.ph[:, 2 * C:3 * C], T.ph[:, C:2 * C].indirect(zl[:, 0:20]), tkk, tzl)
-            tkk = acp(T.ph[:, 3 * C:4 * C], T.ph[:, 2 * C:3 * C].indirect(T.ap[:, 0:20]), tkk, tap)
-        elif not last:
-            tpir = acp(T.pir[:], gat(T.crep, kp), tkp)
         tX = []
         for b in range(3):
             tX.append(vtt(T.xt[:, b:4 * C:4], T.rp[:, pl(b)].indirect(T.ap[:, 0:20]), T.tp[:, pl(b)], Op.add, tr[b], ttp[b], tap))
-            fill(2 if r == 0 else 1)
+            fill(1)
         tX.append(vtt(T.xt[:, 3:4 * C:4], T.rg[:], bank(T.psa, 3), Op.add, trg, pt[3]))
         t_rp = [[tr[0]], [tr[1]], [tr[2]], [tX[3]]]
         t_tq = t_tq + [tr[3]]
+        if not last:
+            if r == 0:
+                tkk = acp(T.ph[:, 2 * C:3 * C], T.ph[:, C:2 * C].indirect(zl[:, 0:20]), tkk, tzl)
+            else:
+                tkk = acp(T.ph[:, 2 * C:3 * C], T.ph[:, 0:C].indirect(T.m2u[:, 0:20]), tph, st[4])
+            tkk = acp(T.ph[:, 3 * C:4 * C], T.ph[:, 2 * C:3 * C].indirect((vl if r else T.ap)[:, 0:20]), tkk, tap)
+            tx_kp = pickx(5 + r, T.ph[:, 3 * C:4 * C], T.ciu[:, 0:20], tkk)
         nq, ns = R("xq", r + 1), R("xs", r + 1)
-        fill(1)
         tx = [vqt(nq[:, h:h + H], ns[:, h:h + H], T.xt[:, 4 * h:4 * (h + H)], *tX) for h in (0, H)]
         if not last:
             n = r + 1
@@ -380,8 +382,10 @@ def rank_program(g, core, T, topo):
     py = [mm(T.psb[:, 512 * h:512 * h + H], T.vq[:], T.vs[:], T.xq3[:, H * h:H * h + H], T.xs3[:, H * h:H * h + H], tx[h], tvq, *t_tq) for h in (0, 1)]
     ty0 = vcp(T.yt[:, 0:H], T.psb[:, 0:H], py[0])
     ty1 = acp(T.yt[:, H:C], T.psb[:, 512:512 + H], py[1])
-    need("A", [ty0, ty1])
-    g.scalar.dma_start(T.y[:], T.yt[:]).then_inc(T.sem.ost, 16)
+    need("S", [ty0])
+    g.sync.dma_start(T.y[:, 0:H], T.yt[:, 0:H]).then_inc(T.sem.ost, 16)
+    need("A", [ty1])
+    g.scalar.dma_start(T.y[:, H:C], T.yt[:, H:C]).then_inc(T.sem.ost, 16)
     need("G", [(q, count[q]) for q in ("V", "A", "P", "G")])
-    g.wait_ge(T.sem.ost, 16 * 7)
+    g.wait_ge(T.sem.ost, 16 * 8)
     g.wait_ge(T.sem.sent, sent[0])

from concourse.bass import DstId, RemoteDMATransfer
from concourse.mybir import dt, AluOpType as Op, ActivationFunctionType as Fn

C = 320
H = C // 2
STEP = [1, 2, 4]
ROUNDS = 3
HZ = 192
S0 = 2.0 ** -70
X4, F32, B16, I32, U16, U8 = "float8_e4m3fn_x4", "float32", "bfloat16", "int32", "uint16", "uint8"

SCRATCH = {}
for _names, _w, _d in (
        ("idf id512 ids", C, F32), ("idb mask keep t16 w1k", C, B16), ("wts", 2 * C, B16), ("pcol qi", 1, I32), ("qf", 1, F32),
        ("c16", 20, F32), ("pk", 8, I32), ("pku", 8, U16), ("fours dia less dib", 16, B16), ("thr inv", 16, F32), ("ein", 516, B16),
        ("eq", 512, X4), ("es", 512, U8),
        ("xin", 4 * C, B16), ("uin vin", 512, B16), ("ci32 mi32 pi32", 20, I32), ("cu mu pu", 20, U16),
        ("wq", 512, X4), ("wsc", 512, U8), ("uq uq2 vq", 128, X4), ("us us2 vs", 128, U8),
        ("crep thb an am pp tpr", C, B16), ("cir w0 pir", C, F32), ("wx", 14 * C, F32), ("ciu ap thu m2u", 20, U16), ("jc jc0", 40, F32),
        ("sc ga gb f0 f1 kco yt rg", C, F32), ("bits zz", 2 * C, B16), ("lst", 80, U16), ("sm", 340, F32), ("mg", 60, I32),
        ("bg", 2 * C, F32), ("ph", 4 * C, B16), ("tb", 4 * C, B16),
        ("tp vp rp", 4 * C, F32), ("tq tk zt xt", 4 * C, B16), ("zq", C, X4), ("zs", C, U8)):
    for _n in _names.split():
        SCRATCH[_n] = ("sbuf", [128, _w], _d)
for _r in range(ROUNDS + 1):
    SCRATCH["xq%d" % _r] = ("sbuf", [128, C], X4)
    SCRATCH["xs%d" % _r] = ("sbuf", [128, C], U8)
for _r in range(ROUNDS):
    SCRATCH["lq%d" % _r] = ("sbuf", [128, C], X4)
    SCRATCH["ls%d" % _r] = ("sbuf", [128, C], U8)
    for _n in ("lk", "lv", "lz", "kp", "vl", "zl"):
        SCRATCH["%s%d" % (_n, _r)] = ("sbuf", [128, 20], U16)
SCRATCH["psa"] = ("psum", [128, 2048], F32)
SCRATCH["psb"] = ("psum", [128, 2048], F32)

LOADS = ["x", "u", "v", "cl", "pl", "ml", "wc", "ws"]
SEMAPHORES = ["V", "A", "P", "G", "sent", "ost"] + ["d" + k for k in LOADS] + ["%s%d" % (k, r) for k in ("arq", "ark", "arv", "arz") for r in range(ROUNDS)]


def rank_program(g, core, T, topo):
    rank = T.rank_of(core)
    if rank is None:
        return
    queues = {"V": g.vector, "A": g.scalar, "P": g.tensor, "G": g, "S": g.sync}
    count = {k: 0 for k in queues}
    seen = {k: {} for k in queues}
    known = {}

    def need(q, deps):
        for sem, val in sorted(set(deps), key=lambda t: -t[1]):
            if seen[q].get(sem, 0) >= val:
                continue
            queues[q].wait_ge(T.sem[sem], val)
            seen[q][sem] = val
            for s2, v2 in known.get((sem, val), {}).items():
                if seen[q].get(s2, 0) < v2:
                    seen[q][s2] = v2

    def run(q, deps, call, *args, **kw):
        need(q, deps)
        call(*args, **kw).then_inc(T.sem[q], 1)
        count[q] += 1
        known[(q, count[q])] = dict(seen[q])
        return (q, count[q])

    def vfill(ap, k): return run("V", (), g.vector.memset, ap, k)
    def vcp(out, in_, *deps): return run("V", deps, g.vector.tensor_copy, out, in_)
    def vtt(out, a, b, op, *deps): return run("V", deps, g.vector.tensor_tensor, out, a, b, op)
    def vts(out, a, s, op, *deps): return run("V", deps, g.vector.tensor_scalar, out, a, s, None, op)
    def vts2(out, a, s, op, s2, op2, *deps): return run("V", deps, g.vector.tensor_scalar, out, a, s, s2, op, op2)
    def vscan(out, w, x, *deps): return run("V", deps, g.vector.tensor_tensor_scan, out, w, x, 0.0, Op.mult, Op.add)
    def vqt(out, sc, x, *deps): return run("V", deps, g.vector.quantize_mx, out, sc, x)
    def acp(out, in_, *deps): return run("A", deps, g.scalar.activation, out, in_, Fn.Copy)
    def asc(out, in_, k, *deps): return run("A", deps, g.scalar.activation, out, in_, Fn.Copy, scale=k)
    def mm(out, w, ws, x, xs, *deps): return run("P", deps, g.tensor.matmul_mx, out, w, ws, x, xs, True, True)

    def load(queue, name, out, in_):
        queue.dma_start(out, in_).then_inc(T.sem["d" + name], 16)
        return ("d" + name, 16)

    def R(name, r): return T["%s%d" % (name, r)]
    def pl(b): return slice(C * b, C * b + C)
    def bank(ps, b): return ps[:, 512 * b:512 * b + C]
    def w128(b): return slice(128 * b, 128 * b + 128)
    def gat(t, lst): return t[:, 0:C].indirect(lst[:, 0:20])

    sent = [0]

    def send(r, out, src, sem, *deps):
        need("G", deps)
        dst = T.cores[(rank + STEP[r]) % len(T.cores)]
        rid, pid, _ = topo.addr(dst)
        eng = topo.engines(core, dst)[:8]
        g.remote_dma(out, src, T.sem[sem], T.sem.sent, pid, rid, sum(1 << e for e in eng))
        sent[0] += len(eng)

    later = []

    def fill(n=99):
        for _ in range(min(n, len(later))):
            later.pop(0)()

    dc = load(g.scalar, "cl", T.ci32[:], T.cl[:])
    dp = load(g.scalar, "pl", T.pi32[:], T.pl[:])
    dm = load(g.scalar, "ml", T.mi32[:], T.ml[:])
    dx = load(g.sync, "x", T.xin[:], T.x[:])
    du = load(g.sync, "u", T.uin[:], T.u[:])
    dwc = load(g.sync, "wc", T.wq[:].bitcast(dt.uint8), T.wc[:])
    dws = load(g.sync, "ws", T.wsc[:], T.ws[:])
    dv = load(g.sync, "v", T.vin[:], T.v[:])

    def iota(buf, pattern, base, cm, flag=True):
        kw = {"allow_small_or_imprecise_dtypes": True} if flag else {}
        return run("G", (), g.iota, buf[:], pattern, base, cm, **kw)
    i_p = iota(T.pcol, [[0, 1]], 0, 1, False)
    i_c = iota(T.c16, [[16, 20]], 0, 0)
    i_t = iota(T.t16, [[0, 20], [1, 16]], 0, 0)
    i_b = iota(T.idb, [[1, C]], -160, 0)
    i_k = iota(T.pk, [[16, 8]], 0, 0, False)
    t_e1 = vfill(T.ein[:], 1.0)
    t_fo = vfill(T.fours[:], 4.0)
    i_e = run("G", [t_e1], g.affine_select, T.ein[:], T.ein[:], [[1, 516]], Op.is_equal, 0.0, -3, -4)
    i_f = iota(T.idf, [[1, C]], 0, 0)
    i_5 = iota(T.id512, [[512, C]], 0, 0)

    tqi = vts(T.qi[:], T.pcol[:], 15, Op.bitwise_and, i_p)
    tqf = vcp(T.qf[:], T.qi[:], tqi)
    tj = vts(T.jc[:, 0:20], T.c16[:], T.qf[:, 0:1], Op.add, i_c, tqf)
    tj0 = vts(T.jc0[:, 20:40], T.c16[:], T.qf[:, 0:1], Op.add, i_c, tqf)
    tmask = vts(T.mask[:], T.t16[:], T.qf[:, 0:1], Op.is_equal, i_t, tqf)
    tkeep = vts(T.keep[:], T.t16[:], 0.0, Op.not_equal, i_t)
    twt = [vts2(T.wts[:, h:h + C], T.t16[:], T.qf[:, 0:1], Op.not_equal, 4.0, Op.mult, i_t, tqf) for h in (0, C)]
    tdi = vts2(T.dia[:], T.t16[:, 0:16], T.qf[:, 0:1], Op.is_equal, 0.6, Op.mult, i_t, tqf)
    tth = vscan(T.thr[:], T.fours[:], T.dia[:], t_fo, tdi)
    tw1 = vts2(T.w1k[:], T.t16[:], T.qf[:, 0:1], Op.is_gt, 1024.0, Op.mult, i_t, tqf)
    tdj = vts2(T.dib[:], T.t16[:, 0:16], T.qf[:, 0:1], Op.is_equal, 1.0 / S0, Op.mult, i_t, tqf)
    t_le = vfill(T.less[:], 2.0 ** -10)
    tinv = vscan(T.inv[:], T.less[:], T.dib[:], t_le, tdj)
    tcu = vcp(T.cu[:], T.ci32[:], dc)
    tj1 = vcp(T.jc0[:, 0:20], T.ci32[:], dc)
    tcrep = acp(T.crep[:], gat(T.idb, T.cu), i_b, tcu)
    tpu = vcp(T.pu[:], T.pi32[:], dp)
    tan = vcp(T.an[:, 0:C].indirect(T.pu[:, 0:20]), T.idb[:], i_b, tpu)
    tmu = vcp(T.mu[:], T.mi32[:], dm)
    tg0 = vcp(T.mg[:, 20:40], T.mi32[:], dm)

    def wrap16(src, off, out, col, *deps):
        s = {}
        def a(): s[1] = vtt(T.tb[:, col:col + C], src.indirect(off), T.mask[:], Op.mult, tmask, *deps)
        def b(): s[2] = vscan(T.tb[:, col + C:col + 2 * C], T.keep[:], T.tb[:, col:col + C], s[1], tkeep)
        def c(): s[3] = vts(out, T.tb[:, col + C + 15:col + 2 * C:16], 160.0, Op.add, s[2])
        return s, a, b, c

    def pickx(i, src, off, *deps):
        return run("A", deps, g.scalar.activation, T.wx[:, 2 * C * i:2 * C * i + C], src.indirect(off), Fn.Identity, bias=160 * S0, scale=S0)

    def scanx(i, src, *deps):
        return vscan(T.wx[:, 2 * C * i + C:2 * C * i + 2 * C], T.w1k[:], src if src is not None else T.wx[:, 2 * C * i:2 * C * i + C], tw1, *deps)

    def readx(i, out, tok):
        return vts2(out, T.wx[:, 2 * C * i + C + 15:2 * C * i + 2 * C:16], T.inv[:, 15:16], Op.mult, 0.05, Op.add, tok, tinv)

    st = {}

    def rest(jc, tjc, tmg):
        mg, sm = T.mg, T.sm
        def s5(): st[5] = vtt(sm[:, 0:40], jc[:], mg[:, 0:40], Op.min, *tmg(), *tjc())
        def s6(): st[6] = vtt(sm[:, 40:80], jc[:], mg[:, 0:40], Op.max, *tmg(), *tjc())
        def s7(): st["l"] = vcp(T.lst[:], sm[:, 0:80], st[5], st[6])
        def s8(): st["d"] = vtt(sm[:, 80:120], jc[:], mg[:, 0:40], Op.subtract, *tmg(), *tjc())
        def s9(): st[9] = vts(sm[:, 120:160], sm[:, 80:120], 0.0, Op.is_lt, st["d"])
        def s10(): st["q"] = vtt(sm[:, 160:180], sm[:, 120:140], sm[:, 140:160], Op.is_equal, st[9])
        return [s5, s6, s8, s7, s9, s10]

    te, tci = [], {}

    def unpacker(b):
        te.append(vqt(T.eq[:, w128(b)], T.es[:, w128(b)], T.ein[:, 3 - b:515 - b], i_e))

    def inverse():
        s = {}
        def o(): s[0] = vcp(T.cir[:, 0:C].indirect(T.cu[:, 0:20]), T.ids[:], tids, tcu)
        def b(): s[2] = scanx(2, T.cir[:], s[0])
        def c(): tci["u"] = readx(2, T.ciu[:], s[2])
        return [o, b, c]

    tx_cm = pickx(0, T.crep[:, 0:C], T.mu[:, 0:20], tcrep, tmu)
    tam = acp(T.am[:], gat(T.an, T.mu), tan, tmu)
    tx_kp = pickx(1, T.am[:, 0:C], T.pu[:, 0:20], tam)
    tx = [vqt(T.xq0[:, h:h + H], T.xs0[:, h:h + H], T.xin[:, 4 * h:4 * (h + H)], dx) for h in (0, H)]
    t_cm = scanx(0, None, tx_cm)
    tpk = vcp(T.pku[:], T.pk[:], i_k)
    tuq = vqt(T.uq[:], T.us[:], T.uin[:], du)
    t_cm = readx(0, T.mg[:, 0:20], t_cm)
    later.extend(rest(T.jc0, lambda: (tj0, tj1), lambda: (t_cm, tg0)))
    fill(2)
    tu1 = vcp(T.uq2[:, 0:128].bitcast(dt.uint32), T.uq[:, 0:128].bitcast(dt.uint32).indirect(T.pku[:, 0:8]), tuq, tpk)
    tu2 = acp(T.us2[:, 0:128], T.us[:, 0:128].indirect(T.pku[:, 0:8]), tuq, tpk)
    tids = asc(T.ids[:], T.idf[:], S0, i_f)
    fill()
    send(0, R("lq", 0)[:, 0:C].bitcast(dt.uint8), T.xq0[:, 0:C].bitcast(dt.uint8), "arq0", *tx)
    send(0, R("ls", 0)[:, 0:C], T.xs0[:, 0:C], "arq0", *tx)

    t_tq, t_rp, tX, tkp, tkk = [], [()] * 4, [], None, None
    for r in range(ROUNDS):
        last = r + 1 == ROUNDS
        xq, xs, lst, sm, mg, vl, zl = R("xq", r), R("xs", r), T.lst, T.sm, T.mg, R("vl", r), R("zl", r)
        lk, lv, lz = R("lk", r), R("lv", r), R("lz", r)
        arq, ark, arv, arz = ("arq%d" % r, 16), ("ark%d" % r, 8), ("arv%d" % r, 8), ("arz%d" % r, 8)

        def own(b): return mm(bank(T.psa, b), T.eq[:, w128(b)], T.es[:, w128(b)], xq[:, 0:C], xs[:, 0:C], te[b], *tx, *t_rp[b])

        ps = [mm(T.psb[:, 512 * h:512 * h + H], T.uq2[:], T.us2[:], xq[:, H * h:H * h + H], xs[:, H * h:H * h + H], tx[h], tu1, tu2, *t_tq) for h in (0, 1)]
        if r:
            pt = [own(b) for b in range(4)]
        fill()
        ts = [vcp(T.sc[:, 0:H], T.psb[:, 0:H], ps[0]), acp(T.sc[:, H:C], T.psb[:, 512:512 + H], ps[1])]
        if r:
            tkp = scanx(4 + r, None, tx_kp)
        tl = st["l"]
        tga = acp(T.ga[:], T.sc[:, 0:C].indirect(lst[:, 20:40]), *ts, tl)
        tgb1 = acp(T.gb[:, H:C], T.sc[:, 0:C].indirect(lst[:, 10:20]), *ts, tl)
        tgb0 = vcp(T.gb[:, 0:H], T.sc[:, 0:C].indirect(lst[:, 0:10]), *ts, tl)
        ttp, kps = {}, {}
        if r:
            tkp = readx(4 + r, R("kp", r)[:], tkp)
            send(r, R("lk", r)[:], R("kp", r)[:], "ark%d" % r, tkp)
            tpir = acp(T.pir[:], gat(T.crep, R("kp", r)), tkp)
            for b in range(3):
                ttp[b] = acp(T.tp[:, pl(b)], bank(T.psa, b), pt[b], *tX)
        else:
            tpp = acp(T.pp[:], gat(T.am, T.pu), tam)
            def q1(): kps[2] = scanx(1, None, tx_kp)
            def q2(): kps[3] = readx(1, R("kp", 0)[:], kps[2])
            later.extend([q1, lambda: unpacker(0), q2] + [lambda b=b: unpacker(b) for b in range(1, 4)])
            fill(1)
        tb0 = vtt(T.bits[:, 0:H], T.sc[:, 0:C].indirect(lst[:, 40:50]), T.gb[:, 0:H], Op.is_le, tgb0)
        tb2 = vtt(T.bits[:, C:2 * C], T.sc[:, 0:C].indirect(lst[:, 60:80]), T.ga[:], Op.is_le, tga)
        tb1 = vtt(T.bits[:, H:C], T.sc[:, 0:C].indirect(lst[:, 50:60]), T.gb[:, H:C], Op.is_le, tgb1)
        fill(1)
        tz = vscan(T.zz[:], T.wts[:], T.bits[:], *twt, tb0, tb1, tb2)
        fill(1)
        e1 = vts(sm[:, 180:220], T.zz[:, 15:2 * C:16], T.thr[:, 15:16], Op.is_ge, tz, tth)
        fill(1)
        e2 = vtt(sm[:, 220:240], sm[:, 180:200], sm[:, 200:220], Op.is_equal, e1)
        fill(1)
        e3 = vtt(sm[:, 240:260], sm[:, 220:240], sm[:, 160:180], Op.is_equal, e2, st["q"])
        fill(1)
        e4 = vtt(sm[:, 260:280], sm[:, 240:260], sm[:, 80:100], Op.mult, e3, st["d"])
        f4 = vtt(sm[:, 300:320], sm[:, 240:260], sm[:, 100:120], Op.mult, e3, st["d"])
        fill(1)
        e5 = vtt(sm[:, 280:300], sm[:, 260:280], mg[:, 0:20], Op.add, e4)
        f5 = vtt(sm[:, 320:340], sm[:, 300:320], mg[:, 20:40], Op.add, f4)
        tvl = vcp(vl[:], sm[:, 280:300], e5)
        tap = vcp(T.ap[:] if r else T.thu[:], sm[:, 320:340], f5)
        if r == 0:
            send(0, R("lk", 0)[:], R("kp", 0)[:], "ark0", kps[3])
        send(r, R("lv", r)[:], vl[:], "arv%d" % r, tvl)

        def neighbour(): return [mm(bank(T.psb, b), T.eq[:, w128(b)], T.es[:, w128(b)], R("lq", r)[:], R("ls", r)[:], arq, *ts) for b in range(4)]
        tq, tk, tv = {}, {}, {}

        def pick(b): tk[b] = acp(T.tk[:, pl(b)], T.tq[:, pl(b)].indirect(lk[:, 0:20]), tq[b], ark)
        def aevac(b): tq[b] = asc(T.tq[:, pl(b)], bank(T.psb, b), 0.5, pq[b])
        def vevac(b): tq[b] = vts(T.tq[:, pl(b)], bank(T.psb, b), 0.5, Op.mult, pq[b])
        def addv(b): tv[b] = vtt(T.vp[:, pl(b)], T.tq[:, pl(b)].indirect(lv[:, 0:20]), T.tk[:, pl(b)], Op.add, tq[b], tk[b], arv)
        def zcols(b, c0, c1): return T.zt[:, 4 * c0 + b:4 * c1:4], T.vp[:, pl(b)].indirect(lz[:, c0 // 16:c1 // 16])

        table = T.idf if last else T.w0

        def next_lists():
            def m(): st["m"] = vtt(T.bg[:, 0:C], gat(T.f1, T.ciu), T.mask[:], Op.mult, tf1, tci["u"])
            def n0(): st[0] = vscan(T.bg[:, C:2 * C], T.keep[:], T.bg[:, 0:C], st["m"])
            def n1(): st[1] = vcp(T.mg[:, 40:60], T.bg[:, C + 15:2 * C:16], st[0])
            def n2(): st[2] = vts(T.mg[:, 0:20], T.mg[:, 40:60], 9, Op.logical_shift_right, st[1])
            def n3(): st[3] = vts(T.mg[:, 20:40], T.mg[:, 40:60], 511, Op.bitwise_and, st[1])
            def n4(): st[4] = vcp(T.m2u[:], T.mg[:, 0:20], st[2])
            return [m, n0, n1, n2] + ([n4] if r else []) + [n3] + rest(T.jc, lambda: (tj, tci["f"]), lambda: (st[2], st[3]))

        if r == 0:
            later.extend(inverse())
            pt = [own(b) for b in range(4)]
            for b in range(3):
                ttp[b] = acp(T.tp[:, pl(b)], bank(T.psa, b), pt[b])
            tt0 = acp(T.tpr[:], gat(T.pp, T.thu), tpp, tap)
            tthb = acp(T.thb[:], gat(T.idb, T.thu), tap)
            pq = neighbour()
            tph = acp(T.ph[:, 0:C], gat(T.idb, vl), tvl, i_b)
            tkk = acp(T.ph[:, C:2 * C], T.ph[:, 0:C].indirect(vl[:, 0:20]), tph)
            aevac(0)
            aevac(1)
            pick(0)
            fill()
            pick(1)
            s, a, b, c = wrap16(T.tpr[:, 0:C], T.ciu[:, 0:20], zl[:], 0, tt0, tci["u"])
            s2, a2, b2, c2 = wrap16(T.thb[:, 0:C], T.ciu[:, 0:20], T.ap[:], 2 * C, tthb, tci["u"])
            a()
            tci["f"] = vcp(T.jc[:, 20:40], T.ciu[:], tci["u"])
            b()
            c()
            tzl = s[3]
            send(0, R("lz", 0)[:], zl[:], "arz0", tzl)
            a2()
            tw0 = vtt(T.w0[:], gat(T.id512, T.cu), T.idf[:], Op.add, i_5, i_f, tcu)
            b2()
            vevac(2)
            c2()
            vevac(3)
            tap = s2[3]
            pick(2)
            pick(3)
            tf0 = acp(T.f0[:], gat(table, vl), tvl, tw0)
        else:
            pq = neighbour()
            fill()
            s, a, b, c = wrap16(T.pir[:, 0:C], vl[:, 0:20], zl[:], 0, tpir, tvl)
            a()
            b()
            c()
            tzl = s[3]
            send(r, R("lz", r)[:], zl[:], "arz%d" % r, tzl)
            tf0 = acp(T.f0[:], gat(table, vl), tvl, tw0, i_f)
            if last:
                tvq = vqt(T.vq[:], T.vs[:], T.vin[:], dv)
            else:
                tph = acp(T.ph[:, 0:C], gat(T.idb, vl), tvl, i_b)
            aevac(0)
            vevac(1)
            pick(0)
            vevac(2)
            pick(1)
            vevac(3)
            pick(2)
            pick(3)
        for b in range(4):
            addv(b)
        t_tq = [tq[b] for b in range(4)]
        za = [acp(*zcols(0, 0, C), tv[0], arz), acp(*zcols(1, 0, C), tv[1]), acp(*zcols(2, 0, HZ), tv[2])]
        zv = [vcp(*zcols(2, HZ, C), tv[2], arz), vcp(*zcols(3, HZ, C), tv[3]), vcp(*zcols(3, 0, HZ), tv[3])]
        tz1 = vqt(T.zq[:, HZ:C], T.zs[:, HZ:C], T.zt[:, 4 * HZ:4 * C], *zv, za[1])
        tz0 = vqt(T.zq[:, 0:HZ], T.zs[:, 0:HZ], T.zt[:, 0:4 * HZ], *zv, *za)
        if last:
            tco = acp(T.kco[:], gat(T.f0, zl), tf0, tzl)
            need("S", [tco])
            g.sync.dma_start(T.co[:], T.kco[0:128:16, :]).then_inc(T.sem.ost, 16)
        else:
            tf1 = acp(T.f1[:], gat(T.f0, zl), tf0, tzl)
            later.extend(next_lists())
        order = [0, 1, 3, 2]
        pr, tr = {}, {}
        for b in order:
            pr[b] = mm(bank(T.psb if b == 3 else T.psa, b), T.wq[:, w128(b)], T.wsc[:, w128(b)], T.zq[:], T.zs[:], dwc, dws, tz0, tz1, tq[3] if b == 3 else ttp[b])
        fill(2)
        for b in order:
            tr[b] = asc(T.rp[:, pl(b)], bank(T.psb if b == 3 else T.psa, b), 0.03125, pr[b], *tX)
        trg = acp(T.rg[:], T.rp[:, pl(3)].indirect(T.ap[:, 0:20]), tr[3], tap)
        tX = []
        for b in range(3):
            tX.append(vtt(T.xt[:, b:4 * C:4], T.rp[:, pl(b)].indirect(T.ap[:, 0:20]), T.tp[:, pl(b)], Op.add, tr[b], ttp[b], tap))
            fill(1)
        tX.append(vtt(T.xt[:, 3:4 * C:4], T.rg[:], bank(T.psa, 3), Op.add, trg, pt[3]))
        t_rp = [[tr[0]], [tr[1]], [tr[2]], [tX[3]]]
        t_tq = t_tq + [tr[3]]
        if not last:
            if r == 0:
                tkk = acp(T.ph[:, 2 * C:3 * C], T.ph[:, C:2 * C].indirect(zl[:, 0:20]), tkk, tzl)
            else:
                tkk = acp(T.ph[:, 2 * C:3 * C], T.ph[:, 0:C].indirect(T.m2u[:, 0:20]), tph, st[4])
            tkk = acp(T.ph[:, 3 * C:4 * C], T.ph[:, 2 * C:3 * C].indirect((vl if r else T.ap)[:, 0:20]), tkk, tap)
            tx_kp = pickx(5 + r, T.ph[:, 3 * C:4 * C], T.ciu[:, 0:20], tkk)
        nq, ns = R("xq", r + 1), R("xs", r + 1)
        tx = [vqt(nq[:, h:h + H], ns[:, h:h + H], T.xt[:, 4 * h:4 * (h + H)], *tX) for h in (0, H)]
        if not last:
            n = r + 1
            send(n, R("lq", n)[:, 0:C].bitcast(dt.uint8), nq[:, 0:C].bitcast(dt.uint8), "arq%d" % n, *tx)
            send(n, R("ls", n)[:, 0:C], ns[:, 0:C], "arq%d" % n, *tx)

    need("S", tx)
    g.sync.dma_start(T.oc[:, 0:4 * C], T.xq3[:, 0:C].bitcast(dt.uint8)).then_inc(T.sem.ost, 16)
    for k in range(4):
        g.sync.dma_start(T.osc[4 * k:4 * k + 4, 0:C], T.xs3[32 * k:32 * k + 4, 0:C]).then_inc(T.sem.ost, 16)
    py = [mm(T.psb[:, 512 * h:512 * h + H], T.vq[:], T.vs[:], T.xq3[:, H * h:H * h + H], T.xs3[:, H * h:H * h + H], tx[h], tvq, *t_tq) for h in (0, 1)]
    ty0 = vcp(T.yt[:, 0:H], T.psb[:, 0:H], py[0])
    ty1 = acp(T.yt[:, H:C], T.psb[:, 512:512 + H], py[1])
    need("S", [ty0])
    g.sync.dma_start(T.y[:, 0:H], T.yt[:, 0:H]).then_inc(T.sem.ost, 16)
    need("A", [ty1])
    g.scalar.dma_start(T.y[:, H:C], T.yt[:, H:C]).then_inc(T.sem.ost, 16)
    need("G", [(q, count[q]) for q in ("V", "A", "P", "G")])
    g.wait_ge(T.sem.ost, 16 * 8)
    g.wait_ge(T.sem.sent, sent[0])
